import numpy as np
import ml_dtypes


def mxq(x, axis, fmt="e4m3"):
    dtype, down = {"e4m3": (ml_dtypes.float8_e4m3fn, 7), "e5m2": (ml_dtypes.float8_e5m2, 14)}[fmt]
    v = np.moveaxis(np.asarray(x, np.float32).astype(ml_dtypes.bfloat16).astype(np.float64), axis, -1)
    blocks = v.reshape(v.shape[:-1] + (-1, 32))
    amax = np.abs(blocks).max(-1, keepdims=True)
    byte = np.maximum(np.where(amax > 0, np.frexp(amax)[1] - 1 + 127, 0) - down, 1)
    scale = np.exp2(byte - 127.0)
    codes = (blocks / scale).astype(np.float32).astype(dtype).astype(np.float64)
    return np.moveaxis((codes * scale).reshape(v.shape), -1, axis)


WIDE = False


def mx_kscale(k):
    if not WIDE:
        return np.ones(k)
    levels = np.array([10, -10, 5, -5, 0])
    if k % 512:
        return np.exp2(np.random.permutation(np.resize(levels, k // 32))).repeat(32)
    a = np.empty((k // 512, 16))
    for p in range(k // 512):
        a[p, :8] = np.random.permutation(np.resize(levels, 8))
        for g in range(8):
            far = levels[np.abs(levels - a[p, g]) >= 10]
            a[p, g + 8] = far[np.random.randint(len(far))]
    return np.exp2(a.ravel()).repeat(32)


def f64(x):
    return np.asarray(x).astype(np.float64)


def striped8(idx):
    return np.concatenate([v.reshape(-1, 16).T for v in idx]).astype(np.uint16)


def unstriped8(offs):
    return np.stack([offs[16 * g:16 * g + 16].T.reshape(-1) for g in range(8)]).astype(np.int64)


E2M1 = np.array([0.0, 0.5, 1.0, 1.5, 2.0, 3.0, 4.0, 6.0, -0.0, -0.5, -1.0, -1.5, -2.0, -3.0, -4.0, -6.0])


def pack_weight(w, fmt):
    k, n = w.shape
    w = f64(np.asarray(w, np.float32).astype(ml_dtypes.bfloat16)).reshape(k // 32, 32, n)
    amax = np.abs(w).max(1)
    if fmt == "e4m3":
        byte = np.frexp(amax)[1] - 1 + 127 - 7
    else:
        mant, ex = np.frexp(amax / 6.0)
        byte = np.where(mant > 0.5, ex, ex - 1) + 127
    byte = np.clip(np.where(amax > 0, byte, 1), 1, 254)
    scaled = (w * np.exp2(127.0 - byte)[:, None, :]).reshape(k, n).astype(np.float32)
    by_word = np.ascontiguousarray(scaled.reshape(k // 512, 128, 4, n).transpose(0, 1, 3, 2))
    if fmt == "e4m3":
        words = by_word.astype(ml_dtypes.float8_e4m3fn).view(np.uint8)
    else:
        c = by_word.astype(ml_dtypes.float4_e2m1fn).view(np.uint8) & 0xF
        words = (c[..., 0::2] | (c[..., 1::2] << 4)).reshape(k // 512, 128, 2 * n)
    return np.ascontiguousarray(words), np.ascontiguousarray(byte.astype(np.uint8).reshape(k // 512, 16, n))


def unpack_weight(words, scales, fmt):
    g, _, n = scales.shape
    words = np.ascontiguousarray(words).reshape(g, 128, n, -1)
    if fmt == "e4m3":
        vals = words.view(ml_dtypes.float8_e4m3fn).astype(np.float64)
    else:
        nib = np.empty((g, 128, n, 4), np.uint8)
        nib[..., 0::2] = words & 0xF
        nib[..., 1::2] = words >> 4
        vals = E2M1[nib]
    vals = vals * np.repeat(np.exp2(scales.astype(np.float64) - 127.0), 8, axis=1)[..., None]
    return vals.transpose(0, 1, 3, 2).reshape(g * 512, n)


def gelu(v):
    return 0.5 * v * (1.0 + np.tanh(np.sqrt(2.0 / np.pi) * (v + 0.044715 * v**3)))


K, M, T, S = 1024, 128, 1024, 512


def setup_inputs():
    n = np.random.standard_normal
    s = mx_kscale(K)[:, None]
    w = n((K, M)) / np.sqrt(K) / s
    w4 = pack_weight(w, "e2m1")
    rest = w - unpack_weight(*w4, "e2m1")
    p_r8 = pack_weight(rest, "e4m3")
    return {
        "xT": (n((K, T)) * s).astype(np.float32),
        "w4_words": w4[0],
        "w4_scales": w4[1],
        "r8_words": p_r8[0],
        "r8_scales": p_r8[1],
        "wgt": np.repeat(np.random.uniform(0.5, 2.0, (8, S)), 16, axis=0).astype(np.float32),
        "b": (0.3 * n(128)).astype(np.float32),
        "wgo": np.repeat(np.random.uniform(0.5, 2.0, (8, S)), 16, axis=0).astype(np.float32),
        "offs": striped8(np.stack([np.random.permutation(T)[:S] for _ in range(8)])),
        "offs2": striped8(np.stack([np.random.permutation(T)[:S] for _ in range(8)])),
    }


def reference(xT, w4_words, w4_scales, r8_words, r8_scales, wgt, b, wgo, offs, offs2):
    idx = unstriped8(offs)
    group = np.arange(K) % 512 // 64
    xg = f64(wgt)[np.arange(K) // 4 % 128] * f64(xT)[np.arange(K)[:, None], idx[group]]
    xT_ = mxq(xg, 0, "e4m3")
    w4_ = unpack_weight(w4_words, w4_scales, "e2m1")
    r8_ = unpack_weight(r8_words, r8_scales, "e4m3")
    y = w4_.T @ xT_ + r8_.T @ xT_
    place = unstriped8(offs2)[np.arange(M) % 128 // 16]
    out = np.zeros((M, T))
    out[np.arange(M)[:, None], place] = f64(wgo)[np.arange(M) % 128] * (gelu(y + f64(b)[:, None]))
    return out

@@ -1,0 +1,177 @@
+from contextlib import ExitStack
+
+import concourse.mybir as mybir
+
+FLOPS = 268435456
+
+F32 = mybir.dt.float32
+BF16 = mybir.dt.bfloat16
+U8 = mybir.dt.uint8
+U16 = mybir.dt.uint16
+U32 = mybir.dt.uint32
+I32 = mybir.dt.int32
+E4M3 = mybir.dt.float8_e4m3fn_x4
+E2M1 = mybir.dt.float4_e2m1fn_x4
+
+MULT = mybir.AluOpType.mult
+COPY = mybir.ActivationFunctionType.Copy
+GELU = mybir.ActivationFunctionType.Gelu_apprx_tanh
+
+P = 128
+T = 1024
+S = 512
+H = 256
+NQ = 128
+PASSES = 2
+PACK = 4
+OC = H // 16
+
+
+def tile_list_hboth_gelu_kernel(
+    tc, xT, w4_words, w4_scales, r8_words, r8_scales, wgt, b, wgo, offs, offs2, out
+):
+    nc = tc.nc
+    with ExitStack() as ctx:
+        keep = ctx.enter_context(tc.tile_pool(name="keep", bufs=1))
+        psum = ctx.enter_context(tc.psum_pool(name="psum", bufs=1))
+
+        offs_t = keep.tile([P, S // 16], U16, name="offs_t")
+        offs2_t = keep.tile([P, S // 16], U16, name="offs2_t")
+        wgt_h = [keep.tile([P, H], F32, name="wgt%d" % h, align_bytes=64) for h in range(2)]
+        wgo_t = keep.tile([P, S], F32, name="wgo_t", align_bytes=64)
+        b_t = keep.tile([P, 1], F32, name="b_t")
+        dummy = keep.tile([P, 1], F32, name="dummy")
+        w4_t = keep.tile([P, PASSES, 2 * P], U8, name="w4_t", align_bytes=64)
+        r8_t = keep.tile([P, PASSES, P * PACK], U8, name="r8_t", align_bytes=64)
+        sc_t = keep.tile([P, 2 * PASSES * P], U8, name="sc_t", align_bytes=64)
+        out_t = keep.tile([P, T], F32, name="out_t", align_bytes=64)
+        planes = [
+            [keep.tile([P, T], F32, name="x%d%d" % (a, i), align_bytes=64) for i in range(PACK)]
+            for a in range(PASSES)
+        ]
+
+        nc.vector.memset(dummy[:], 0.0)
+        nc.vector.memset(sc_t[:].bitcast(I32), 0)
+        nc.vector.memset(out_t[:], 0.0)
+        warm = keep.tile([P, 1], F32, name="warm")
+        nc.scalar.activation(warm[:], dummy[:], GELU)
+
+        x_view = xT.rearrange("(a p i) t -> a i p t", a=PASSES, p=P, i=PACK)
+        nc.sync.dma_start(out=planes[0][0][:], in_=x_view[0, 0])
+        nc.scalar.dma_start(out=wgt_h[0][:], in_=wgt[:, 0:H])
+        nc.sync.dma_start(out=offs_t[:], in_=offs)
+        nc.sync.dma_start(out=wgt_h[1][:], in_=wgt[:, H:S])
+        for n in range(1, 4):
+            nc.sync.dma_start(out=planes[n // PACK][n % PACK][:], in_=x_view[n // PACK, n % PACK])
+        for which, scales in enumerate((w4_scales, r8_scales)):
+            cols = slice(which * PASSES * P, (which + 1) * PASSES * P)
+            for q in range(4):
+                nc.scalar.dma_start(
+                    out=sc_t[32 * q : 32 * q + 4, cols].rearrange("r (a n) -> r a n", a=PASSES).bitcast(I32),
+                    in_=scales[:, 4 * q : 4 * q + 4, :].rearrange("a r n -> r a n").bitcast(I32),
+                )
+        for n in range(4, PASSES * PACK):
+            if n == 6:
+                nc.sync.dma_start(out=offs2_t[:], in_=offs2)
+            nc.sync.dma_start(out=planes[n // PACK][n % PACK][:], in_=x_view[n // PACK, n % PACK])
+        nc.sync.dma_start(out=b_t[:], in_=b.rearrange("(p o) -> p o", o=1))
+        nc.sync.dma_start(
+            out=r8_t[:].bitcast(I32), in_=r8_words.rearrange("a p n i -> p a (n i)").bitcast(I32)
+        )
+        nc.sync.dma_start(out=w4_t[:].bitcast(I32), in_=w4_words.rearrange("a p n -> p a n").bitcast(I32))
+        nc.sync.dma_start(out=wgo_t[:], in_=wgo)
+
+        acc = [psum.tile([P, NQ], F32, name="acc%d" % q) for q in range(4)]
+        val = [keep.tile([P, H], F32, name="val%d" % h, align_bytes=64) for h in range(2)]
+
+        def gather(g, a, i, j0, j1):
+            h = j0 // H
+            nc.vector.tensor_tensor(
+                g[:, i, j0 - h * H : j1 - h * H],
+                planes[a][i][:].indirect(offs_t[:, j0 // 16 : j1 // 16]),
+                wgt_h[h][:, j0 - h * H : j1 - h * H],
+                MULT,
+            )
+
+        def interleave(g, a, j0, j1, on_vector):
+            h = j0 // H
+            xb = keep.tile([P, (j1 - j0) * PACK], BF16, name="xb%d_%d" % (a, j0), align_bytes=64)
+            dst = xb[:].rearrange("p (c i t) -> p c t i", i=4, t=PACK)
+            src = g[:, :, j0 - h * H : j1 - h * H].rearrange("p t (c i) -> p c t i", i=4)
+            if on_vector:
+                nc.vector.tensor_copy(dst, src)
+            else:
+                nc.scalar.activation(dst, src, COPY)
+            return xb
+
+        def quantise(xb, a, j0, j1):
+            codes = keep.tile([P, j1 - j0], U32, name="codes%d_%d" % (a, j0), align_bytes=64)
+            scales = keep.tile([P, j1 - j0], U8, name="scales%d_%d" % (a, j0), align_bytes=64)
+            nc.vector.quantize_mx(out=codes[:].bitcast(E4M3), scales=scales[:], in_=xb[:])
+            return codes, scales
+
+        def multiply(a, j0, j1, codes, scales):
+            for j in range(j0, j1, NQ):
+                cols = slice(j - j0, j - j0 + NQ)
+                nc.tensor.matmul_mx(
+                    out=acc[j // NQ][:],
+                    lhsT=w4_t[:, a, :].bitcast(E2M1),
+                    lhsT_scale=sc_t[:, a * P : (a + 1) * P],
+                    rhs=codes[:, cols].bitcast(E4M3),
+                    rhs_scale=scales[:, cols],
+                    start=(a == 0),
+                    stop=False,
+                )
+                nc.tensor.matmul_mx(
+                    out=acc[j // NQ][:],
+                    lhsT=r8_t[:, a, :].bitcast(E4M3),
+                    lhsT_scale=sc_t[:, (PASSES + a) * P : (PASSES + a + 1) * P],
+                    rhs=codes[:, cols].bitcast(E4M3),
+                    rhs_scale=scales[:, cols],
+                    start=False,
+                    stop=(a == PASSES - 1),
+                )
+
+        def gelu(h):
+            for s in range(2):
+                nc.scalar.activation(
+                    val[h][:, s * NQ : (s + 1) * NQ], acc[2 * h + s][:], GELU, bias=b_t[:, 0:1]
+                )
+
+        def scatter(h):
+            nc.vector.tensor_tensor(
+                out_t[:].indirect(offs2_t[:, h * OC : (h + 1) * OC]),
+                val[h][:],
+                wgo_t[:, h * H : (h + 1) * H],
+                MULT,
+            )
+
+        g = {
+            (h, a): keep.tile([P, PACK, H], F32, name="g%d%d" % (h, a), align_bytes=64)
+            for h in range(2)
+            for a in range(PASSES)
+        }
+        for h in range(2):
+            for i in range(PACK):
+                gather(g[h, 0], 0, i, h * H, (h + 1) * H)
+            xb = interleave(g[h, 0], 0, h * H, (h + 1) * H, False)
+            multiply(0, h * H, (h + 1) * H, *quantise(xb, 0, h * H, (h + 1) * H))
+        for i in range(PACK):
+            gather(g[0, 1], 1, i, 0, H)
+        xb = interleave(g[0, 1], 1, 0, H, False)
+        multiply(1, 0, H, *quantise(xb, 1, 0, H))
+        gelu(0)
+        for i in range(PACK - 1):
+            gather(g[1, 1], 1, i, H, S)
+        mid = H + NQ
+        gather(g[1, 1], 1, PACK - 1, H, mid)
+        xb2 = interleave(g[1, 1], 1, H, mid, False)
+        gather(g[1, 1], 1, PACK - 1, mid, S)
+        xb3 = interleave(g[1, 1], 1, mid, S, True)
+        multiply(1, H, mid, *quantise(xb2, 1, H, mid))
+        multiply(1, mid, S, *quantise(xb3, 1, mid, S))
+        scatter(0)
+        gelu(1)
+        scatter(1)
+        nc.sync.dma_start(out=out[:, 0:S], in_=out_t[:, 0:S])
+        nc.scalar.dma_start(out=out[:, S:T], in_=out_t[:, S:T])

@@ -24,7 +24,7 @@ H = 256
 NQ = 128
 PASSES = 2
 PACK = 4
-OC = H // 16
+EARLY = S - NQ
 
 
 def tile_list_hboth_gelu_kernel(
@@ -37,7 +37,8 @@ def tile_list_hboth_gelu_kernel(
 
         offs_t = keep.tile([P, S // 16], U16, name="offs_t")
         offs2_t = keep.tile([P, S // 16], U16, name="offs2_t")
-        wgt_h = [keep.tile([P, H], F32, name="wgt%d" % h, align_bytes=64) for h in range(2)]
+        rows = keep.tile([P, PACK + 1, S], F32, name="rows", align_bytes=64)
+        wgt_t = rows[:, 0, :]
         wgo_t = keep.tile([P, S], F32, name="wgo_t", align_bytes=64)
         b_t = keep.tile([P, 1], F32, name="b_t")
         dummy = keep.tile([P, 1], F32, name="dummy")
@@ -50,68 +51,84 @@ def tile_list_hboth_gelu_kernel(
             for a in range(PASSES)
         ]
 
-        nc.vector.memset(dummy[:], 0.0)
         nc.vector.memset(sc_t[:].bitcast(I32), 0)
+        nc.vector.memset(dummy[:], 0.0)
         nc.vector.memset(out_t[:], 0.0)
+
         warm = keep.tile([P, 1], F32, name="warm")
         nc.scalar.activation(warm[:], dummy[:], GELU)
 
         x_view = xT.rearrange("(a p i) t -> a i p t", a=PASSES, p=P, i=PACK)
-        nc.sync.dma_start(out=planes[0][0][:], in_=x_view[0, 0])
-        nc.scalar.dma_start(out=wgt_h[0][:], in_=wgt[:, 0:H])
-        nc.sync.dma_start(out=offs_t[:], in_=offs)
-        nc.sync.dma_start(out=wgt_h[1][:], in_=wgt[:, H:S])
-        for n in range(1, 4):
+
+        def load_plane(n):
             nc.sync.dma_start(out=planes[n // PACK][n % PACK][:], in_=x_view[n // PACK, n % PACK])
-        for which, scales in enumerate((w4_scales, r8_scales)):
-            cols = slice(which * PASSES * P, (which + 1) * PASSES * P)
-            for q in range(4):
-                nc.scalar.dma_start(
+
+        def load_scales(q, engine):
+            for which, scales in enumerate((w4_scales, r8_scales)):
+                cols = slice(which * PASSES * P, (which + 1) * PASSES * P)
+                engine.dma_start(
                     out=sc_t[32 * q : 32 * q + 4, cols].rearrange("r (a n) -> r a n", a=PASSES).bitcast(I32),
                     in_=scales[:, 4 * q : 4 * q + 4, :].rearrange("a r n -> r a n").bitcast(I32),
                 )
-        for n in range(4, PASSES * PACK):
-            if n == 6:
-                nc.sync.dma_start(out=offs2_t[:], in_=offs2)
-            nc.sync.dma_start(out=planes[n // PACK][n % PACK][:], in_=x_view[n // PACK, n % PACK])
+
+        def load_words():
+            nc.sync.dma_start(
+                out=r8_t[:].bitcast(I32), in_=r8_words.rearrange("a p n i -> p a (n i)").bitcast(I32)
+            )
+            nc.sync.dma_start(out=w4_t[:].bitcast(I32), in_=w4_words.rearrange("a p n -> p a n").bitcast(I32))
+
+        load_plane(0)
+        nc.scalar.dma_start(out=wgt_t[:, 0:NQ], in_=wgt[:, 0:NQ])
+        nc.sync.dma_start(out=offs_t[:], in_=offs)
+        nc.sync.dma_start(out=wgt_t[:, NQ:S], in_=wgt[:, NQ:S])
+        load_plane(1)
+        load_plane(2)
+        load_scales(0, nc.sync)
+        load_scales(1, nc.sync)
+        for n in range(3, 7):
+            load_plane(n)
+        load_scales(2, nc.sync)
+        load_plane(7)
+        load_scales(3, nc.sync)
         nc.sync.dma_start(out=b_t[:], in_=b.rearrange("(p o) -> p o", o=1))
-        nc.sync.dma_start(
-            out=r8_t[:].bitcast(I32), in_=r8_words.rearrange("a p n i -> p a (n i)").bitcast(I32)
-        )
-        nc.sync.dma_start(out=w4_t[:].bitcast(I32), in_=w4_words.rearrange("a p n -> p a n").bitcast(I32))
+        nc.sync.dma_start(out=offs2_t[:], in_=offs2)
+        load_words()
         nc.sync.dma_start(out=wgo_t[:], in_=wgo)
 
         acc = [psum.tile([P, NQ], F32, name="acc%d" % q) for q in range(4)]
-        val = [keep.tile([P, H], F32, name="val%d" % h, align_bytes=64) for h in range(2)]
+        val = keep.tile([P, S], F32, name="val", align_bytes=64)
+        picked0 = keep.tile([P, PACK, S], F32, name="picked0", align_bytes=64)
 
-        def gather(g, a, i, j0, j1):
-            h = j0 // H
+        def place(a, j0, j1):
+            if a == 0:
+                return picked0[:, :, j0:j1]
+            if j0 < EARLY:
+                return rows[:, 1 : PACK + 1, j0:j1]
+            return rows[:, 0:PACK, j0 - EARLY : j1 - EARLY]
+
+        def gather(a, i, j0, j1):
             nc.vector.tensor_tensor(
-                g[:, i, j0 - h * H : j1 - h * H],
+                place(a, j0, j1)[:, i, :],
                 planes[a][i][:].indirect(offs_t[:, j0 // 16 : j1 // 16]),
-                wgt_h[h][:, j0 - h * H : j1 - h * H],
+                wgt_t[:, j0:j1],
                 MULT,
             )
 
-        def interleave(g, a, j0, j1, on_vector):
-            h = j0 // H
-            xb = keep.tile([P, (j1 - j0) * PACK], BF16, name="xb%d_%d" % (a, j0), align_bytes=64)
+        def interleave(a, j0, j1, tag=None):
+            xb = keep.tile([P, (j1 - j0) * PACK], BF16, name="xb%d_%d" % (a, j0), tag=tag or "xb%d_%d" % (a, j0), align_bytes=64)
             dst = xb[:].rearrange("p (c i t) -> p c t i", i=4, t=PACK)
-            src = g[:, :, j0 - h * H : j1 - h * H].rearrange("p t (c i) -> p c t i", i=4)
-            if on_vector:
-                nc.vector.tensor_copy(dst, src)
-            else:
-                nc.scalar.activation(dst, src, COPY)
+            src = place(a, j0, j1).rearrange("p t (c i) -> p c t i", i=4)
+            nc.scalar.activation(dst, src, COPY)
             return xb
 
-        def quantise(xb, a, j0, j1):
-            codes = keep.tile([P, j1 - j0], U32, name="codes%d_%d" % (a, j0), align_bytes=64)
+        def quantise(xb, a, j0, j1, tag=None):
+            codes = keep.tile([P, j1 - j0], U32, name="codes%d_%d" % (a, j0), tag=tag or "codes%d_%d" % (a, j0), align_bytes=64)
             scales = keep.tile([P, j1 - j0], U8, name="scales%d_%d" % (a, j0), align_bytes=64)
             nc.vector.quantize_mx(out=codes[:].bitcast(E4M3), scales=scales[:], in_=xb[:])
             return codes, scales
 
-        def multiply(a, j0, j1, codes, scales):
-            for j in range(j0, j1, NQ):
+        def multiply(a, j, j0, codes, scales):
+            if True:
                 cols = slice(j - j0, j - j0 + NQ)
                 nc.tensor.matmul_mx(
                     out=acc[j // NQ][:],
@@ -132,46 +149,52 @@ def tile_list_hboth_gelu_kernel(
                     stop=(a == PASSES - 1),
                 )
 
-        def gelu(h):
-            for s in range(2):
-                nc.scalar.activation(
-                    val[h][:, s * NQ : (s + 1) * NQ], acc[2 * h + s][:], GELU, bias=b_t[:, 0:1]
-                )
+        def gelu(q):
+            nc.scalar.activation(val[:, q * NQ : (q + 1) * NQ], acc[q][:], GELU, bias=b_t[:, 0:1])
 
-        def scatter(h):
+        def scatter(j0, j1):
             nc.vector.tensor_tensor(
-                out_t[:].indirect(offs2_t[:, h * OC : (h + 1) * OC]),
-                val[h][:],
-                wgo_t[:, h * H : (h + 1) * H],
-                MULT,
+                out_t[:].indirect(offs2_t[:, j0 // 16 : j1 // 16]), val[:, j0:j1], wgo_t[:, j0:j1], MULT
             )
 
-        g = {
-            (h, a): keep.tile([P, PACK, H], F32, name="g%d%d" % (h, a), align_bytes=64)
-            for h in range(2)
-            for a in range(PASSES)
-        }
-        for h in range(2):
-            for i in range(PACK):
-                gather(g[h, 0], 0, i, h * H, (h + 1) * H)
-            xb = interleave(g[h, 0], 0, h * H, (h + 1) * H, False)
-            multiply(0, h * H, (h + 1) * H, *quantise(xb, 0, h * H, (h + 1) * H))
-        for i in range(PACK):
-            gather(g[0, 1], 1, i, 0, H)
-        xb = interleave(g[0, 1], 1, 0, H, False)
-        multiply(1, 0, H, *quantise(xb, 1, 0, H))
+        def finish(xb, q):
+            late = quantise(xb, 1, q * NQ, (q + 1) * NQ)
+            multiply(0, q * NQ, q // 2 * H, *early[q // 2])
+            multiply(1, q * NQ, q * NQ, *late)
+
+        gather(0, 0, 0, NQ)
+        gather(0, 0, NQ, S)
+        gather(0, 1, 0, S)
+        gather(0, 2, 0, S)
+        gather(0, 3, H, S)
+        xb_late = interleave(0, H, S)
+        gather(0, 3, 0, H)
+        xb = interleave(0, 0, H)
+        gather(1, 0, 0, EARLY)
+        early = {1: quantise(xb_late, 0, H, S)}
+        gather(1, 1, 0, EARLY)
+        early[0] = quantise(xb, 0, 0, H)
+        gather(1, 2, 0, EARLY)
+        gather(1, 3, 0, NQ)
+        xb0 = interleave(1, 0, NQ)
+        gather(1, 3, NQ, EARLY)
+        xb1 = interleave(1, NQ, H)
+        gather(1, 0, EARLY, S)
+        finish(xb0, 0)
+        xb2 = interleave(1, H, EARLY)
         gelu(0)
-        for i in range(PACK - 1):
-            gather(g[1, 1], 1, i, H, S)
-        mid = H + NQ
-        gather(g[1, 1], 1, PACK - 1, H, mid)
-        xb2 = interleave(g[1, 1], 1, H, mid, False)
-        gather(g[1, 1], 1, PACK - 1, mid, S)
-        xb3 = interleave(g[1, 1], 1, mid, S, True)
-        multiply(1, H, mid, *quantise(xb2, 1, H, mid))
-        multiply(1, mid, S, *quantise(xb3, 1, mid, S))
-        scatter(0)
+        gather(1, 1, EARLY, S)
+        finish(xb1, 1)
+        gather(1, 2, EARLY, S)
+        gather(1, 3, EARLY, S)
+        finish(xb2, 2)
         gelu(1)
-        scatter(1)
+        xb3 = interleave(1, EARLY, S, "codes1_0")
+        scatter(0, NQ)
+        finish(xb3, 3)
+        gelu(2)
+        gelu(3)
+        scatter(NQ, EARLY)
+        scatter(EARLY, S)
         nc.sync.dma_start(out=out[:, 0:S], in_=out_t[:, 0:S])
         nc.scalar.dma_start(out=out[:, S:T], in_=out_t[:, S:T])

@@ -39,19 +39,18 @@ def tile_list_hboth_gelu_kernel(
         offs2_t = keep.tile([P, S // 16], U16, name="offs2_t")
         rows = keep.tile([P, PACK + 1, S], F32, name="rows", align_bytes=64)
         wgt_t = rows[:, 0, :]
-        wgo_t = keep.tile([P, S], F32, name="wgo_t", align_bytes=64)
         b_t = keep.tile([P, 1], F32, name="b_t")
         dummy = keep.tile([P, 1], F32, name="dummy")
         w4_t = keep.tile([P, PASSES, 2 * P], U8, name="w4_t", align_bytes=64)
         r8_t = keep.tile([P, PASSES, P * PACK], U8, name="r8_t", align_bytes=64)
-        sc_t = keep.tile([P, 2 * PASSES * P], U8, name="sc_t", align_bytes=64)
+        sc_t = keep.tile([P, 2 * PASSES, 4 * P], U8, name="sc_t", align_bytes=64)
         out_t = keep.tile([P, T], F32, name="out_t", align_bytes=64)
         planes = [
             [keep.tile([P, T], F32, name="x%d%d" % (a, i), align_bytes=64) for i in range(PACK)]
             for a in range(PASSES)
         ]
 
-        nc.vector.memset(sc_t[:].bitcast(I32), 0)
+        nc.vector.memset(sc_t[:, :, 0:P].bitcast(I32), 0)
         nc.vector.memset(dummy[:], 0.0)
         nc.vector.memset(out_t[:], 0.0)
 
@@ -63,12 +62,17 @@ def tile_list_hboth_gelu_kernel(
         def load_plane(n):
             nc.sync.dma_start(out=planes[n // PACK][n % PACK][:], in_=x_view[n // PACK, n % PACK])
 
-        def load_scales(q, engine):
+        def load_scales():
             for which, scales in enumerate((w4_scales, r8_scales)):
-                cols = slice(which * PASSES * P, (which + 1) * PASSES * P)
-                engine.dma_start(
-                    out=sc_t[32 * q : 32 * q + 4, cols].rearrange("r (a n) -> r a n", a=PASSES).bitcast(I32),
-                    in_=scales[:, 4 * q : 4 * q + 4, :].rearrange("a r n -> r a n").bitcast(I32),
+                nc.sync.dma_start(
+                    out=sc_t[0:P:32, which * PASSES : (which + 1) * PASSES, :].bitcast(I32),
+                    in_=scales.rearrange("a (q r) n -> q a (r n)", r=4).bitcast(I32),
+                )
+
+        def deal_scales():
+            for r in range(1, 4):
+                nc.sync.dma_start(
+                    out=sc_t[r:P:32, :, 0:P].bitcast(I32), in_=sc_t[0:P:32, :, r * P : (r + 1) * P].bitcast(I32)
                 )
 
         def load_words():
@@ -83,17 +87,13 @@ def tile_list_hboth_gelu_kernel(
         nc.sync.dma_start(out=wgt_t[:, NQ:S], in_=wgt[:, NQ:S])
         load_plane(1)
         load_plane(2)
-        load_scales(0, nc.sync)
-        load_scales(1, nc.sync)
-        for n in range(3, 7):
+        load_scales()
+        for n in range(3, 8):
             load_plane(n)
-        load_scales(2, nc.sync)
-        load_plane(7)
-        load_scales(3, nc.sync)
         nc.sync.dma_start(out=b_t[:], in_=b.rearrange("(p o) -> p o", o=1))
         nc.sync.dma_start(out=offs2_t[:], in_=offs2)
         load_words()
-        nc.sync.dma_start(out=wgo_t[:], in_=wgo)
+        deal_scales()
 
         acc = [psum.tile([P, NQ], F32, name="acc%d" % q) for q in range(4)]
         val = keep.tile([P, S], F32, name="val", align_bytes=64)
@@ -133,7 +133,7 @@ def tile_list_hboth_gelu_kernel(
                 nc.tensor.matmul_mx(
                     out=acc[j // NQ][:],
                     lhsT=w4_t[:, a, :].bitcast(E2M1),
-                    lhsT_scale=sc_t[:, a * P : (a + 1) * P],
+                    lhsT_scale=sc_t[:, a, 0:P],
                     rhs=codes[:, cols].bitcast(E4M3),
                     rhs_scale=scales[:, cols],
                     start=(a == 0),
@@ -142,7 +142,7 @@ def tile_list_hboth_gelu_kernel(
                 nc.tensor.matmul_mx(
                     out=acc[j // NQ][:],
                     lhsT=r8_t[:, a, :].bitcast(E4M3),
-                    lhsT_scale=sc_t[:, (PASSES + a) * P : (PASSES + a + 1) * P],
+                    lhsT_scale=sc_t[:, PASSES + a, 0:P],
                     rhs=codes[:, cols].bitcast(E4M3),
                     rhs_scale=scales[:, cols],
                     start=False,
@@ -164,6 +164,8 @@ def tile_list_hboth_gelu_kernel(
 
         gather(0, 0, 0, NQ)
         gather(0, 0, NQ, S)
+        wgo_t = keep.tile([P, S], F32, name="wgo_t", tag="x00", align_bytes=64)
+        nc.sync.dma_start(out=wgo_t[:], in_=wgo)
         gather(0, 1, 0, S)
         gather(0, 2, 0, S)
         gather(0, 3, H, S)
@@ -192,9 +194,9 @@ def tile_list_hboth_gelu_kernel(
         xb3 = interleave(1, EARLY, S, "codes1_0")
         scatter(0, NQ)
         finish(xb3, 3)
+        scatter(NQ, H)
         gelu(2)
         gelu(3)
-        scatter(NQ, EARLY)
-        scatter(EARLY, S)
+        scatter(H, S)
         nc.sync.dma_start(out=out[:, 0:S], in_=out_t[:, 0:S])
         nc.scalar.dma_start(out=out[:, S:T], in_=out_t[:, S:T])

@@ -37,10 +37,10 @@ def tile_list_hboth_gelu_kernel(
 
         offs_t = keep.tile([P, S // 16], U16, name="offs_t")
         offs2_t = keep.tile([P, S // 16], U16, name="offs2_t")
-        rows = keep.tile([P, PACK + 1, S], F32, name="rows", align_bytes=64)
-        wgt_t = rows[:, 0, :]
+        wgt_t = keep.tile([P, S], F32, name="wgt_t", align_bytes=64)
+        wgt_first = keep.tile([P, NQ], F32, name="wgt_first", tag="codes0_0", align_bytes=64)
+        picked1 = keep.tile([P, PACK, EARLY], F32, name="picked1", align_bytes=64)
         b_t = keep.tile([P, 1], F32, name="b_t")
-        dummy = keep.tile([P, 1], F32, name="dummy")
         w4_t = keep.tile([P, PASSES, 2 * P], U8, name="w4_t", align_bytes=64)
         r8_t = keep.tile([P, PASSES, P * PACK], U8, name="r8_t", align_bytes=64)
         sc_t = keep.tile([P, 2 * PASSES, 4 * P], U8, name="sc_t", align_bytes=64)
@@ -51,11 +51,10 @@ def tile_list_hboth_gelu_kernel(
         ]
 
         nc.vector.memset(sc_t[:, :, 0:P].bitcast(I32), 0)
-        nc.vector.memset(dummy[:], 0.0)
         nc.vector.memset(out_t[:], 0.0)
 
         warm = keep.tile([P, 1], F32, name="warm")
-        nc.scalar.activation(warm[:], dummy[:], GELU)
+        nc.scalar.activation(warm[:], out_t[:, 0:1], GELU)
 
         x_view = xT.rearrange("(a p i) t -> a i p t", a=PASSES, p=P, i=PACK)
 
@@ -82,7 +81,8 @@ def tile_list_hboth_gelu_kernel(
             nc.sync.dma_start(out=w4_t[:].bitcast(I32), in_=w4_words.rearrange("a p n -> p a n").bitcast(I32))
 
         load_plane(0)
-        nc.scalar.dma_start(out=wgt_t[:, 0:NQ], in_=wgt[:, 0:NQ])
+        nc.scalar.dma_start(out=wgt_first[:], in_=wgt[:, 0:NQ])
+        nc.scalar.copy(wgt_t[:, 0:NQ], wgt_first[:])
         nc.sync.dma_start(out=offs_t[:], in_=offs)
         nc.sync.dma_start(out=wgt_t[:, NQ:S], in_=wgt[:, NQ:S])
         load_plane(1)
@@ -102,15 +102,13 @@ def tile_list_hboth_gelu_kernel(
         def place(a, j0, j1):
             if a == 0:
                 return picked0[:, :, j0:j1]
-            if j0 < EARLY:
-                return rows[:, 1 : PACK + 1, j0:j1]
-            return rows[:, 0:PACK, j0 - EARLY : j1 - EARLY]
+            return picked1[:, :, j0 % EARLY : j0 % EARLY + j1 - j0]
 
         def gather(a, i, j0, j1):
             nc.vector.tensor_tensor(
                 place(a, j0, j1)[:, i, :],
                 planes[a][i][:].indirect(offs_t[:, j0 // 16 : j1 // 16]),
-                wgt_t[:, j0:j1],
+                wgt_first[:] if j1 == NQ else wgt_t[:, j0:j1],
                 MULT,
             )
 
@@ -122,7 +120,7 @@ def tile_list_hboth_gelu_kernel(
             return xb
 
         def quantise(xb, a, j0, j1, tag=None):
-            codes = keep.tile([P, j1 - j0], U32, name="codes%d_%d" % (a, j0), tag=tag or "codes%d_%d" % (a, j0), align_bytes=64)
+            codes = keep.tile([P, j1 - j0], U32, name="codes%d_%d" % (a, j0), align_bytes=64)
             scales = keep.tile([P, j1 - j0], U8, name="scales%d_%d" % (a, j0), align_bytes=64)
             nc.vector.quantize_mx(out=codes[:].bitcast(E4M3), scales=scales[:], in_=xb[:])
             return codes, scales
@@ -159,7 +157,7 @@ def tile_list_hboth_gelu_kernel(
 
         def finish(xb, q):
             late = quantise(xb, 1, q * NQ, (q + 1) * NQ)
-            multiply(0, q * NQ, q // 2 * H, *early[q // 2])
+            multiply(0, q * NQ, 0, *early)
             multiply(1, q * NQ, q * NQ, *late)
 
         gather(0, 0, 0, NQ)
@@ -168,27 +166,22 @@ def tile_list_hboth_gelu_kernel(
         nc.sync.dma_start(out=wgo_t[:], in_=wgo)
         gather(0, 1, 0, S)
         gather(0, 2, 0, S)
-        gather(0, 3, H, S)
-        xb_late = interleave(0, H, S)
-        gather(0, 3, 0, H)
-        xb = interleave(0, 0, H)
+        gather(0, 3, 0, S)
+        xb = interleave(0, 0, S)
         gather(1, 0, 0, EARLY)
-        early = {1: quantise(xb_late, 0, H, S)}
         gather(1, 1, 0, EARLY)
-        early[0] = quantise(xb, 0, 0, H)
         gather(1, 2, 0, EARLY)
         gather(1, 3, 0, NQ)
         xb0 = interleave(1, 0, NQ)
         gather(1, 3, NQ, EARLY)
         xb1 = interleave(1, NQ, H)
-        gather(1, 0, EARLY, S)
+        early = quantise(xb, 0, 0, S)
         finish(xb0, 0)
         xb2 = interleave(1, H, EARLY)
         gelu(0)
-        gather(1, 1, EARLY, S)
+        for i in range(PACK):
+            gather(1, i, EARLY, S)
         finish(xb1, 1)
-        gather(1, 2, EARLY, S)
-        gather(1, 3, EARLY, S)
         finish(xb2, 2)
         gelu(1)
         xb3 = interleave(1, EARLY, S, "codes1_0")

@@ -191,5 +191,4 @@ def tile_list_hboth_gelu_kernel(
         gelu(2)
         gelu(3)
         scatter(H, S)
-        nc.sync.dma_start(out=out[:, 0:S], in_=out_t[:, 0:S])
-        nc.scalar.dma_start(out=out[:, S:T], in_=out_t[:, S:T])
+        nc.sync.dma_start(out=out, in_=out_t[:])

@@ -39,7 +39,7 @@ def tile_list_hboth_gelu_kernel(
         offs2_t = keep.tile([P, S // 16], U16, name="offs2_t")
         wgt_t = keep.tile([P, S], F32, name="wgt_t", align_bytes=64)
         wgt_first = keep.tile([P, NQ], F32, name="wgt_first", tag="codes0_0", align_bytes=64)
-        picked1 = keep.tile([P, PACK, EARLY], F32, name="picked1", align_bytes=64)
+        picked1 = keep.tile([P, PACK, S], F32, name="picked1", align_bytes=64)
         b_t = keep.tile([P, 1], F32, name="b_t")
         w4_t = keep.tile([P, PASSES, 2 * P], U8, name="w4_t", align_bytes=64)
         r8_t = keep.tile([P, PASSES, P * PACK], U8, name="r8_t", align_bytes=64)
@@ -100,13 +100,12 @@ def tile_list_hboth_gelu_kernel(
         picked0 = keep.tile([P, PACK, S], F32, name="picked0", align_bytes=64)
 
         def place(a, j0, j1):
-            if a == 0:
-                return picked0[:, :, j0:j1]
-            return picked1[:, :, j0 % EARLY : j0 % EARLY + j1 - j0]
+            return (picked0, picked1)[a][:, :, j0:j1]
 
         def gather(a, i, j0, j1):
+            c0 = 0 if j0 == EARLY else j0
             nc.vector.tensor_tensor(
-                place(a, j0, j1)[:, i, :],
+                place(a, c0, c0 + j1 - j0)[:, i, :],
                 planes[a][i][:].indirect(offs_t[:, j0 // 16 : j1 // 16]),
                 wgt_first[:] if j1 == NQ else wgt_t[:, j0:j1],
                 MULT,
@@ -117,6 +116,14 @@ def tile_list_hboth_gelu_kernel(
             dst = xb[:].rearrange("p (c i t) -> p c t i", i=4, t=PACK)
             src = place(a, j0, j1).rearrange("p t (c i) -> p c t i", i=4)
             nc.scalar.activation(dst, src, COPY)
+            return xb
+
+        def interleave_last(tag):
+            xb = keep.tile([P, NQ * PACK], BF16, name="xb_last", tag=tag, align_bytes=64)
+            dst = xb[:].rearrange("p (c i u v) -> p c u v i", i=4, u=2, v=2)
+            flat = picked1[:].rearrange("p t s -> p (t s)")[:, EARLY : EARLY + 2 * (S + NQ)]
+            src = flat.rearrange("p (u w c i) -> p c u w i", u=2, w=5, i=4)[:, :, :, 0:5:4, :]
+            nc.scalar.copy(dst, src)
             return xb
 
         def quantise(xb, a, j0, j1, tag=None):
@@ -168,8 +175,8 @@ def tile_list_hboth_gelu_kernel(
         gather(0, 2, 0, S)
         gather(0, 3, 0, S)
         xb = interleave(0, 0, S)
-        gather(1, 0, 0, EARLY)
-        gather(1, 1, 0, EARLY)
+        gather(1, 0, 0, S)
+        gather(1, 1, 0, S)
         gather(1, 2, 0, EARLY)
         gather(1, 3, 0, NQ)
         xb0 = interleave(1, 0, NQ)
@@ -179,16 +186,16 @@ def tile_list_hboth_gelu_kernel(
         finish(xb0, 0)
         xb2 = interleave(1, H, EARLY)
         gelu(0)
-        for i in range(PACK):
+        for i in range(2, PACK):
             gather(1, i, EARLY, S)
         finish(xb1, 1)
         finish(xb2, 2)
         gelu(1)
-        xb3 = interleave(1, EARLY, S, "codes1_0")
+        xb3 = interleave_last("codes1_0")
         scatter(0, NQ)
         finish(xb3, 3)
-        scatter(NQ, H)
         gelu(2)
+        scatter(NQ, EARLY)
         gelu(3)
-        scatter(H, S)
+        scatter(EARLY, S)
         nc.sync.dma_start(out=out, in_=out_t[:])

@@ -99,13 +99,14 @@ def tile_list_hboth_gelu_kernel(
         val = keep.tile([P, S], F32, name="val", align_bytes=64)
         picked0 = keep.tile([P, PACK, S], F32, name="picked0", align_bytes=64)
 
+        last = picked1[:].rearrange("p t s -> p (t s)")[:, EARLY : EARLY + S].rearrange("p (t s) -> p t s", t=PACK)
+
         def place(a, j0, j1):
             return (picked0, picked1)[a][:, :, j0:j1]
 
         def gather(a, i, j0, j1):
-            c0 = 0 if j0 == EARLY else j0
             nc.vector.tensor_tensor(
-                place(a, c0, c0 + j1 - j0)[:, i, :],
+                last[:, i, :] if j0 == EARLY else place(a, j0, j1)[:, i, :],
                 planes[a][i][:].indirect(offs_t[:, j0 // 16 : j1 // 16]),
                 wgt_first[:] if j1 == NQ else wgt_t[:, j0:j1],
                 MULT,
@@ -120,10 +121,8 @@ def tile_list_hboth_gelu_kernel(
 
         def interleave_last(tag):
             xb = keep.tile([P, NQ * PACK], BF16, name="xb_last", tag=tag, align_bytes=64)
-            dst = xb[:].rearrange("p (c i u v) -> p c u v i", i=4, u=2, v=2)
-            flat = picked1[:].rearrange("p t s -> p (t s)")[:, EARLY : EARLY + 2 * (S + NQ)]
-            src = flat.rearrange("p (u w c i) -> p c u w i", u=2, w=5, i=4)[:, :, :, 0:5:4, :]
-            nc.scalar.copy(dst, src)
+            dst = xb[:].rearrange("p (c i t) -> p c t i", i=4, t=PACK)
+            nc.scalar.activation(dst, last.rearrange("p t (c i) -> p c t i", i=4), COPY)
             return xb
 
         def quantise(xb, a, j0, j1, tag=None):
@@ -132,7 +131,7 @@ def tile_list_hboth_gelu_kernel(
             nc.vector.quantize_mx(out=codes[:].bitcast(E4M3), scales=scales[:], in_=xb[:])
             return codes, scales
 
-        def multiply(a, j, j0, codes, scales):
+        def multiply(a, j, j0, codes, scales, first):
             if True:
                 cols = slice(j - j0, j - j0 + NQ)
                 nc.tensor.matmul_mx(
@@ -141,7 +140,7 @@ def tile_list_hboth_gelu_kernel(
                     lhsT_scale=sc_t[:, a, 0:P],
                     rhs=codes[:, cols].bitcast(E4M3),
                     rhs_scale=scales[:, cols],
-                    start=(a == 0),
+                    start=first,
                     stop=False,
                 )
                 nc.tensor.matmul_mx(
@@ -151,7 +150,7 @@ def tile_list_hboth_gelu_kernel(
                     rhs=codes[:, cols].bitcast(E4M3),
                     rhs_scale=scales[:, cols],
                     start=False,
-                    stop=(a == PASSES - 1),
+                    stop=not first,
                 )
 
         def gelu(q):
@@ -164,8 +163,12 @@ def tile_list_hboth_gelu_kernel(
 
         def finish(xb, q):
             late = quantise(xb, 1, q * NQ, (q + 1) * NQ)
-            multiply(0, q * NQ, 0, *early)
-            multiply(1, q * NQ, q * NQ, *late)
+            if q < 3:
+                multiply(0, q * NQ, 0, *early, True)
+                multiply(1, q * NQ, q * NQ, *late, False)
+            else:
+                multiply(1, q * NQ, q * NQ, *late, True)
+                multiply(0, q * NQ, 0, *early, False)
 
         gather(0, 0, 0, NQ)
         gather(0, 0, NQ, S)
@@ -176,7 +179,7 @@ def tile_list_hboth_gelu_kernel(
         gather(0, 3, 0, S)
         xb = interleave(0, 0, S)
         gather(1, 0, 0, S)
-        gather(1, 1, 0, S)
+        gather(1, 1, 0, EARLY)
         gather(1, 2, 0, EARLY)
         gather(1, 3, 0, NQ)
         xb0 = interleave(1, 0, NQ)
@@ -186,9 +189,10 @@ def tile_list_hboth_gelu_kernel(
         finish(xb0, 0)
         xb2 = interleave(1, H, EARLY)
         gelu(0)
-        for i in range(2, PACK):
-            gather(1, i, EARLY, S)
+        gather(1, 1, EARLY, S)
+        gather(1, 2, EARLY, S)
         finish(xb1, 1)
+        gather(1, 3, EARLY, S)
         finish(xb2, 2)
         gelu(1)
         xb3 = interleave_last("codes1_0")

@@ -20,11 +20,10 @@ GELU = mybir.ActivationFunctionType.Gelu_apprx_tanh
 P = 128
 T = 1024
 S = 512
-H = 256
 NQ = 128
 PASSES = 2
 PACK = 4
-EARLY = S - NQ
+W = NQ * PACK
 
 
 def tile_list_hboth_gelu_kernel(
@@ -35,50 +34,32 @@ def tile_list_hboth_gelu_kernel(
         keep = ctx.enter_context(tc.tile_pool(name="keep", bufs=1))
         psum = ctx.enter_context(tc.psum_pool(name="psum", bufs=1))
 
+        def tile(name, shape, dtype, tag=None):
+            return keep.tile(shape, dtype, name=name, tag=tag or name, align_bytes=64)
+
         offs_t = keep.tile([P, S // 16], U16, name="offs_t")
         offs2_t = keep.tile([P, S // 16], U16, name="offs2_t")
-        wgt_t = keep.tile([P, S], F32, name="wgt_t", align_bytes=64)
-        wgt_first = keep.tile([P, NQ], F32, name="wgt_first", tag="codes0_0", align_bytes=64)
-        picked1 = keep.tile([P, PACK, S], F32, name="picked1", align_bytes=64)
         b_t = keep.tile([P, 1], F32, name="b_t")
-        w4_t = keep.tile([P, PASSES, 2 * P], U8, name="w4_t", align_bytes=64)
-        r8_t = keep.tile([P, PASSES, P * PACK], U8, name="r8_t", align_bytes=64)
-        sc_t = keep.tile([P, 2 * PASSES, 4 * P], U8, name="sc_t", align_bytes=64)
-        out_t = keep.tile([P, T], F32, name="out_t", align_bytes=64)
-        planes = [
-            [keep.tile([P, T], F32, name="x%d%d" % (a, i), align_bytes=64) for i in range(PACK)]
-            for a in range(PASSES)
-        ]
+        wgt_t = tile("wgt_t", [P, S], F32)
+        wgt_first = tile("wgt_first", [P, NQ], F32)
+        w4_t = tile("w4_t", [P, PASSES, 2 * P], U8)
+        r8_t = tile("r8_t", [P, PASSES, P * PACK], U8)
+        sc_t = tile("sc_t", [P, 2 * PASSES, 4 * P], U8)
+        page = tile("page", [P, T], F32)
+        planes = [tile("plane%d" % n, [P, T], F32) for n in range(PASSES * PACK)]
+        picked = [tile("picked%d" % a, [P, PACK, S], F32) for a in range(PASSES)]
+        val = tile("val", [P, S], F32)
+        sums = [psum.tile([P, NQ], F32, name="sum%d" % q) for q in range(4)]
 
         nc.vector.memset(sc_t[:, :, 0:P].bitcast(I32), 0)
-        nc.vector.memset(out_t[:], 0.0)
-
+        nc.vector.memset(page[:], 0.0)
         warm = keep.tile([P, 1], F32, name="warm")
-        nc.scalar.activation(warm[:], out_t[:, 0:1], GELU)
+        nc.scalar.activation(warm[:], page[:, 0:1], GELU)
 
         x_view = xT.rearrange("(a p i) t -> a i p t", a=PASSES, p=P, i=PACK)
 
         def load_plane(n):
-            nc.sync.dma_start(out=planes[n // PACK][n % PACK][:], in_=x_view[n // PACK, n % PACK])
-
-        def load_scales():
-            for which, scales in enumerate((w4_scales, r8_scales)):
-                nc.sync.dma_start(
-                    out=sc_t[0:P:32, which * PASSES : (which + 1) * PASSES, :].bitcast(I32),
-                    in_=scales.rearrange("a (q r) n -> q a (r n)", r=4).bitcast(I32),
-                )
-
-        def deal_scales():
-            for r in range(1, 4):
-                nc.sync.dma_start(
-                    out=sc_t[r:P:32, :, 0:P].bitcast(I32), in_=sc_t[0:P:32, :, r * P : (r + 1) * P].bitcast(I32)
-                )
-
-        def load_words():
-            nc.sync.dma_start(
-                out=r8_t[:].bitcast(I32), in_=r8_words.rearrange("a p n i -> p a (n i)").bitcast(I32)
-            )
-            nc.sync.dma_start(out=w4_t[:].bitcast(I32), in_=w4_words.rearrange("a p n -> p a n").bitcast(I32))
+            nc.sync.dma_start(out=planes[n][:], in_=x_view[n // PACK, n % PACK])
 
         load_plane(0)
         nc.scalar.dma_start(out=wgt_first[:], in_=wgt[:, 0:NQ])
@@ -87,119 +68,112 @@ def tile_list_hboth_gelu_kernel(
         nc.sync.dma_start(out=wgt_t[:, NQ:S], in_=wgt[:, NQ:S])
         load_plane(1)
         load_plane(2)
-        load_scales()
+        for which, scales in enumerate((w4_scales, r8_scales)):
+            nc.sync.dma_start(
+                out=sc_t[0:P:32, which * PASSES : (which + 1) * PASSES, :].bitcast(I32),
+                in_=scales.rearrange("a (q r) n -> q a (r n)", r=4).bitcast(I32),
+            )
         for n in range(3, 8):
             load_plane(n)
         nc.sync.dma_start(out=b_t[:], in_=b.rearrange("(p o) -> p o", o=1))
         nc.sync.dma_start(out=offs2_t[:], in_=offs2)
-        load_words()
-        deal_scales()
+        nc.sync.dma_start(out=r8_t[:].bitcast(I32), in_=r8_words.rearrange("a p n i -> p a (n i)").bitcast(I32))
+        nc.sync.dma_start(out=w4_t[:].bitcast(I32), in_=w4_words.rearrange("a p n -> p a n").bitcast(I32))
+        for r in range(1, 4):
+            nc.sync.dma_start(
+                out=sc_t[r:P:32, :, 0:P].bitcast(I32), in_=sc_t[0:P:32, :, r * P : (r + 1) * P].bitcast(I32)
+            )
 
-        acc = [psum.tile([P, NQ], F32, name="acc%d" % q) for q in range(4)]
-        val = keep.tile([P, S], F32, name="val", align_bytes=64)
-        picked0 = keep.tile([P, PACK, S], F32, name="picked0", align_bytes=64)
-
-        last = picked1[:].rearrange("p t s -> p (t s)")[:, EARLY : EARLY + S].rearrange("p (t s) -> p t s", t=PACK)
-
-        def place(a, j0, j1):
-            return (picked0, picked1)[a][:, :, j0:j1]
-
-        def gather(a, i, j0, j1):
+        def gather(n, q0, q1, dst=None, weights=None):
+            j0, j1 = q0 * NQ, q1 * NQ
             nc.vector.tensor_tensor(
-                last[:, i, :] if j0 == EARLY else place(a, j0, j1)[:, i, :],
-                planes[a][i][:].indirect(offs_t[:, j0 // 16 : j1 // 16]),
-                wgt_first[:] if j1 == NQ else wgt_t[:, j0:j1],
+                picked[n // PACK][:, n % PACK, j0:j1] if dst is None else dst,
+                planes[n][:].indirect(offs_t[:, j0 // 16 : j1 // 16]),
+                wgt_t[:, j0:j1] if weights is None else weights,
                 MULT,
             )
 
-        def interleave(a, j0, j1, tag=None):
-            xb = keep.tile([P, (j1 - j0) * PACK], BF16, name="xb%d_%d" % (a, j0), tag=tag or "xb%d_%d" % (a, j0), align_bytes=64)
-            dst = xb[:].rearrange("p (c i t) -> p c t i", i=4, t=PACK)
-            src = place(a, j0, j1).rearrange("p t (c i) -> p c t i", i=4)
-            nc.scalar.activation(dst, src, COPY)
-            return xb
+        def weave(dst, src, t0):
+            rows = src.shape[1]
+            nc.scalar.activation(
+                dst.rearrange("p (c i t) -> p c t i", i=4, t=PACK)[:, :, t0 : t0 + rows, :],
+                src.rearrange("p t (c i) -> p c t i", i=4),
+                COPY,
+            )
 
-        def interleave_last(tag):
-            xb = keep.tile([P, NQ * PACK], BF16, name="xb_last", tag=tag, align_bytes=64)
-            dst = xb[:].rearrange("p (c i t) -> p c t i", i=4, t=PACK)
-            nc.scalar.activation(dst, last.rearrange("p t (c i) -> p c t i", i=4), COPY)
-            return xb
-
-        def quantise(xb, a, j0, j1, tag=None):
-            codes = keep.tile([P, j1 - j0], U32, name="codes%d_%d" % (a, j0), align_bytes=64)
-            scales = keep.tile([P, j1 - j0], U8, name="scales%d_%d" % (a, j0), align_bytes=64)
-            nc.vector.quantize_mx(out=codes[:].bitcast(E4M3), scales=scales[:], in_=xb[:])
+        def quantise(src, name, tag=None):
+            n = src.shape[1] // PACK
+            codes = tile("codes_" + name, [P, n], U32, tag)
+            scales = tile("scales_" + name, [P, n], U8)
+            nc.vector.quantize_mx(out=codes[:].bitcast(E4M3), scales=scales[:], in_=src)
             return codes, scales
 
-        def multiply(a, j, j0, codes, scales, first):
-            if True:
-                cols = slice(j - j0, j - j0 + NQ)
+        def multiply(a, q, operand, c0=0):
+            codes, scales = operand
+            cols = slice(c0, c0 + NQ)
+            for which, words in enumerate((w4_t[:, a, :].bitcast(E2M1), r8_t[:, a, :].bitcast(E4M3))):
                 nc.tensor.matmul_mx(
-                    out=acc[j // NQ][:],
-                    lhsT=w4_t[:, a, :].bitcast(E2M1),
-                    lhsT_scale=sc_t[:, a, 0:P],
+                    out=sums[q][:],
+                    lhsT=words,
+                    lhsT_scale=sc_t[:, which * PASSES + a, 0:P],
                     rhs=codes[:, cols].bitcast(E4M3),
                     rhs_scale=scales[:, cols],
-                    start=first,
-                    stop=False,
-                )
-                nc.tensor.matmul_mx(
-                    out=acc[j // NQ][:],
-                    lhsT=r8_t[:, a, :].bitcast(E4M3),
-                    lhsT_scale=sc_t[:, PASSES + a, 0:P],
-                    rhs=codes[:, cols].bitcast(E4M3),
-                    rhs_scale=scales[:, cols],
-                    start=False,
-                    stop=not first,
+                    start=a == 0 and which == 0,
+                    stop=a == 1 and which == 1,
                 )
 
         def gelu(q):
-            nc.scalar.activation(val[:, q * NQ : (q + 1) * NQ], acc[q][:], GELU, bias=b_t[:, 0:1])
+            nc.scalar.activation(val[:, q * NQ : (q + 1) * NQ], sums[q][:], GELU, bias=b_t[:, 0:1])
 
-        def scatter(j0, j1):
+        def scatter(q0, q1):
+            j0, j1 = q0 * NQ, q1 * NQ
             nc.vector.tensor_tensor(
-                out_t[:].indirect(offs2_t[:, j0 // 16 : j1 // 16]), val[:, j0:j1], wgo_t[:, j0:j1], MULT
+                page[:].indirect(offs2_t[:, j0 // 16 : j1 // 16]), val[:, j0:j1], wgo_t[:, j0:j1], MULT
             )
 
-        def finish(xb, q):
-            late = quantise(xb, 1, q * NQ, (q + 1) * NQ)
-            if q < 3:
-                multiply(0, q * NQ, 0, *early, True)
-                multiply(1, q * NQ, q * NQ, *late, False)
-            else:
-                multiply(1, q * NQ, q * NQ, *late, True)
-                multiply(0, q * NQ, 0, *early, False)
+        def cols(q0, q1):
+            return slice(q0 * NQ, q1 * NQ)
 
-        gather(0, 0, 0, NQ)
-        gather(0, 0, NQ, S)
-        wgo_t = keep.tile([P, S], F32, name="wgo_t", tag="x00", align_bytes=64)
+        gather(0, 0, 1, weights=wgt_first[:])
+        gather(0, 1, 4)
+        wgo_t = tile("wgo_t", [P, S], F32, "plane0")
         nc.sync.dma_start(out=wgo_t[:], in_=wgo)
-        gather(0, 1, 0, S)
-        gather(0, 2, 0, S)
-        gather(0, 3, 0, S)
-        xb = interleave(0, 0, S)
-        gather(1, 0, 0, S)
-        gather(1, 1, 0, EARLY)
-        gather(1, 2, 0, EARLY)
-        gather(1, 3, 0, NQ)
-        xb0 = interleave(1, 0, NQ)
-        gather(1, 3, NQ, EARLY)
-        xb1 = interleave(1, NQ, H)
-        early = quantise(xb, 0, 0, S)
-        finish(xb0, 0)
-        xb2 = interleave(1, H, EARLY)
+        woven0 = tile("woven0", [P, 4 * W], BF16)
+        gather(1, 0, 4)
+        weave(woven0[:], picked[0][:, 0:2, :], 0)
+        gather(2, 0, 4)
+        gather(3, 0, 4)
+        weave(woven0[:, 0:W], picked[0][:, 2:4, cols(0, 1)], 2)
+        weave(woven0[:, W : 4 * W], picked[0][:, 2:4, cols(1, 4)], 2)
+        gather(4, 0, 4)
+        early = quantise(woven0[:, 0:W], "00")
+        multiply(0, 0, early)
+        gather(5, 0, 2)
+        gather(5, 2, 4)
+        woven1 = [tile("woven1%d" % q, [P, W], BF16) for q in range(4)]
+        for q in range(4):
+            weave(woven1[q][:], picked[1][:, 0:2, cols(q, q + 1)], 0)
+        gather(6, 0, 3)
+        gather(7, 0, 1, weights=wgt_first[:])
+        weave(woven1[0][:], picked[1][:, 2:4, cols(0, 1)], 2)
+        gather(7, 1, 2)
+        weave(woven1[1][:], picked[1][:, 2:4, cols(1, 2)], 2)
+        middle = quantise(woven0[:, W : 3 * W], "01", "wgt_first")
+        gather(7, 2, 4)
+        weave(woven1[2][:], picked[1][:, 2:4, cols(2, 3)], 2)
+        multiply(0, 1, middle)
+        multiply(0, 2, middle, NQ)
+        multiply(1, 0, quantise(woven1[0][:], "10"))
+        held = picked[1][:, 3, :].rearrange("p (q s) -> p q s", s=NQ)[:, 0:4:3, :]
+        gather(6, 3, 4, dst=held[:, 0, :])
+        weave(woven1[3][:], held, 2)
         gelu(0)
-        gather(1, 1, EARLY, S)
-        gather(1, 2, EARLY, S)
-        finish(xb1, 1)
-        gather(1, 3, EARLY, S)
-        finish(xb2, 2)
-        gelu(1)
-        xb3 = interleave_last("codes1_0")
-        scatter(0, NQ)
-        finish(xb3, 3)
-        gelu(2)
-        scatter(NQ, EARLY)
-        gelu(3)
-        scatter(EARLY, S)
-        nc.sync.dma_start(out=out, in_=out_t[:])
+        multiply(0, 3, quantise(woven0[:, 3 * W : 4 * W], "03", "woven10"))
+        multiply(1, 1, quantise(woven1[1][:], "11"))
+        multiply(1, 2, quantise(woven1[2][:], "12"))
+        multiply(1, 3, quantise(woven1[3][:], "13"))
+        for q in range(1, 4):
+            gelu(q)
+        scatter(0, 1)
+        scatter(1, 4)
+        nc.sync.dma_start(out=out, in_=page[:])

@@ -47,7 +47,8 @@ def tile_list_hboth_gelu_kernel(
         sc_t = tile("sc_t", [P, 2 * PASSES, 4 * P], U8)
         page = tile("page", [P, T], F32)
         planes = [tile("plane%d" % n, [P, T], F32) for n in range(PASSES * PACK)]
-        picked = [tile("picked%d" % a, [P, PACK, S], F32) for a in range(PASSES)]
+        flat1 = tile("flat1", [P, 16 * NQ], F32)
+        picked = [tile("picked0", [P, PACK, S], F32), flat1[:, 0 : PACK * S].rearrange("p (t s) -> p t s", t=PACK)]
         val = tile("val", [P, S], F32)
         sums = [psum.tile([P, NQ], F32, name="sum%d" % q) for q in range(4)]
 
@@ -138,42 +139,50 @@ def tile_list_hboth_gelu_kernel(
         gather(0, 1, 4)
         wgo_t = tile("wgo_t", [P, S], F32, "plane0")
         nc.sync.dma_start(out=wgo_t[:], in_=wgo)
+        wgt_again = tile("wgt_again", [P, NQ], F32)
+        nc.scalar.copy(wgt_again[:], wgt_first[:])
+        for n in range(1, 4):
+            gather(n, 0, 4)
         woven0 = tile("woven0", [P, 4 * W], BF16)
-        gather(1, 0, 4)
-        weave(woven0[:], picked[0][:, 0:2, :], 0)
-        gather(2, 0, 4)
-        gather(3, 0, 4)
-        weave(woven0[:, 0:W], picked[0][:, 2:4, cols(0, 1)], 2)
-        weave(woven0[:, W : 4 * W], picked[0][:, 2:4, cols(1, 4)], 2)
-        gather(4, 0, 4)
-        early = quantise(woven0[:, 0:W], "00")
+        weave(woven0[:, 0 : 2 * W], picked[0][:, :, cols(0, 2)], 0)
+        weave(woven0[:, 2 * W : 4 * W], picked[0][:, :, cols(2, 4)], 0)
+        last = flat1[:, 10 * NQ :].rearrange("p (v u s) -> p v u s", v=2, s=NQ)[:, :, 0:3:2, :]
+        gather(4, 0, 3)
+        gather(5, 0, 1, weights=wgt_first[:])
+        gather(5, 1, 3)
+        early = quantise(woven0[:, 0 : 2 * W], "00", "wgt_first")
         multiply(0, 0, early)
-        gather(5, 0, 2)
-        gather(5, 2, 4)
-        woven1 = [tile("woven1%d" % q, [P, W], BF16) for q in range(4)]
-        for q in range(4):
+        multiply(0, 1, early, NQ)
+        woven1 = [tile("woven1%d" % q, [P, W], BF16) for q in range(3)]
+        for q in range(3):
             weave(woven1[q][:], picked[1][:, 0:2, cols(q, q + 1)], 0)
         gather(6, 0, 3)
-        gather(7, 0, 1, weights=wgt_first[:])
+        gather(7, 0, 1, weights=wgt_again[:])
         weave(woven1[0][:], picked[1][:, 2:4, cols(0, 1)], 2)
         gather(7, 1, 2)
         weave(woven1[1][:], picked[1][:, 2:4, cols(1, 2)], 2)
-        middle = quantise(woven0[:, W : 3 * W], "01", "wgt_first")
         gather(7, 2, 4)
         weave(woven1[2][:], picked[1][:, 2:4, cols(2, 3)], 2)
-        multiply(0, 1, middle)
-        multiply(0, 2, middle, NQ)
+        third = quantise(woven0[:, 2 * W : 3 * W], "02", "wgt_again")
         multiply(1, 0, quantise(woven1[0][:], "10"))
-        held = picked[1][:, 3, :].rearrange("p (q s) -> p q s", s=NQ)[:, 0:4:3, :]
-        gather(6, 3, 4, dst=held[:, 0, :])
-        weave(woven1[3][:], held, 2)
+        multiply(0, 2, third)
         gelu(0)
-        multiply(0, 3, quantise(woven0[:, 3 * W : 4 * W], "03", "woven10"))
+        gather(5, 3, 4, dst=last[:, 0, 1, :])
+        gather(6, 3, 4, dst=last[:, 1, 0, :])
+        gather(4, 3, 4, dst=last[:, 0, 0, :])
         multiply(1, 1, quantise(woven1[1][:], "11"))
         multiply(1, 2, quantise(woven1[2][:], "12"))
-        multiply(1, 3, quantise(woven1[3][:], "13"))
-        for q in range(1, 4):
-            gelu(q)
+        woven_last = tile("woven_last", [P, W], BF16, "codes_10")
+        nc.scalar.copy(
+            woven_last[:].rearrange("p (c i v u) -> p c v u i", i=4, v=2, u=2),
+            last.rearrange("p v u (c i) -> p c v u i", i=4),
+        )
+        gelu(1)
+        gelu(2)
         scatter(0, 1)
-        scatter(1, 4)
+        multiply(0, 3, quantise(woven0[:, 3 * W : 4 * W], "03", "flat1"))
+        multiply(1, 3, quantise(woven_last[:], "13"))
+        scatter(1, 3)
+        gelu(3)
+        scatter(3, 4)
         nc.sync.dma_start(out=out, in_=page[:])

@@ -41,14 +41,23 @@ def tile_list_hboth_gelu_kernel(
         offs2_t = keep.tile([P, S // 16], U16, name="offs2_t")
         b_t = keep.tile([P, 1], F32, name="b_t")
         wgt_t = tile("wgt_t", [P, S], F32)
-        wgt_first = tile("wgt_first", [P, NQ], F32)
         w4_t = tile("w4_t", [P, PASSES, 2 * P], U8)
         r8_t = tile("r8_t", [P, PASSES, P * PACK], U8)
         sc_t = tile("sc_t", [P, 2 * PASSES, 4 * P], U8)
         page = tile("page", [P, T], F32)
         planes = [tile("plane%d" % n, [P, T], F32) for n in range(PASSES * PACK)]
-        flat1 = tile("flat1", [P, 16 * NQ], F32)
-        picked = [tile("picked0", [P, PACK, S], F32), flat1[:, 0 : PACK * S].rearrange("p (t s) -> p t s", t=PACK)]
+        picked0 = tile("picked0", [P, PACK, S], F32)
+        flat = tile("slots", [P, 17 * NQ], F32)
+
+        def slot(s0, n=1):
+            return flat[:, s0 * NQ : (s0 + n) * NQ]
+
+        def pair(s0, s1):
+            lo, step = min(s0, s1), abs(s1 - s0)
+            rows = slot(lo, 2 * step).rearrange("p (t s) -> p t s", t=2)[:, :, 0:NQ]
+            return rows if s0 < s1 else rows[:, ::-1, :]
+
+        wgt_first = tile("wgt_first", [P, NQ], F32)
         val = tile("val", [P, S], F32)
         sums = [psum.tile([P, NQ], F32, name="sum%d" % q) for q in range(4)]
 
@@ -85,19 +94,18 @@ def tile_list_hboth_gelu_kernel(
                 out=sc_t[r:P:32, :, 0:P].bitcast(I32), in_=sc_t[0:P:32, :, r * P : (r + 1) * P].bitcast(I32)
             )
 
-        def gather(n, q0, q1, dst=None, weights=None):
+        def gather(n, q0, q1, dst, weights=None):
             j0, j1 = q0 * NQ, q1 * NQ
             nc.vector.tensor_tensor(
-                picked[n // PACK][:, n % PACK, j0:j1] if dst is None else dst,
+                dst,
                 planes[n][:].indirect(offs_t[:, j0 // 16 : j1 // 16]),
                 wgt_t[:, j0:j1] if weights is None else weights,
                 MULT,
             )
 
         def weave(dst, src, t0):
-            rows = src.shape[1]
             nc.scalar.activation(
-                dst.rearrange("p (c i t) -> p c t i", i=4, t=PACK)[:, :, t0 : t0 + rows, :],
+                dst.rearrange("p (c i t) -> p c t i", i=4, t=PACK)[:, :, t0 : t0 + src.shape[1], :],
                 src.rearrange("p t (c i) -> p c t i", i=4),
                 COPY,
             )
@@ -132,47 +140,37 @@ def tile_list_hboth_gelu_kernel(
                 page[:].indirect(offs2_t[:, j0 // 16 : j1 // 16]), val[:, j0:j1], wgo_t[:, j0:j1], MULT
             )
 
-        def cols(q0, q1):
-            return slice(q0 * NQ, q1 * NQ)
-
-        gather(0, 0, 1, weights=wgt_first[:])
-        gather(0, 1, 4)
+        gather(0, 0, 1, picked0[:, 0, 0:NQ], weights=wgt_first[:])
+        gather(0, 1, 4, picked0[:, 0, NQ:S])
         wgo_t = tile("wgo_t", [P, S], F32, "plane0")
         nc.sync.dma_start(out=wgo_t[:], in_=wgo)
-        wgt_again = tile("wgt_again", [P, NQ], F32)
-        nc.scalar.copy(wgt_again[:], wgt_first[:])
-        for n in range(1, 4):
-            gather(n, 0, 4)
         woven0 = tile("woven0", [P, 4 * W], BF16)
-        weave(woven0[:, 0 : 2 * W], picked[0][:, :, cols(0, 2)], 0)
-        weave(woven0[:, 2 * W : 4 * W], picked[0][:, :, cols(2, 4)], 0)
-        last = flat1[:, 10 * NQ :].rearrange("p (v u s) -> p v u s", v=2, s=NQ)[:, :, 0:3:2, :]
-        gather(4, 0, 3)
-        gather(5, 0, 1, weights=wgt_first[:])
-        gather(5, 1, 3)
-        early = quantise(woven0[:, 0 : 2 * W], "00", "wgt_first")
-        multiply(0, 0, early)
-        multiply(0, 1, early, NQ)
+        for n in range(1, 4):
+            gather(n, 0, 4, picked0[:, n, :])
+        weave(woven0[:], picked0[:], 0)
+        gather(4, 0, 4, slot(5, 4))
+        gather(5, 0, 4, slot(0, 4))
         woven1 = [tile("woven1%d" % q, [P, W], BF16) for q in range(3)]
         for q in range(3):
-            weave(woven1[q][:], picked[1][:, 0:2, cols(q, q + 1)], 0)
-        gather(6, 0, 3)
-        gather(7, 0, 1, weights=wgt_again[:])
-        weave(woven1[0][:], picked[1][:, 2:4, cols(0, 1)], 2)
-        gather(7, 1, 2)
-        weave(woven1[1][:], picked[1][:, 2:4, cols(1, 2)], 2)
-        gather(7, 2, 4)
-        weave(woven1[2][:], picked[1][:, 2:4, cols(2, 3)], 2)
-        third = quantise(woven0[:, 2 * W : 3 * W], "02", "wgt_again")
+            weave(woven1[q][:], pair(q + 5, q), 0)
+        gather(6, 0, 3, slot(11, 3))
+        gather(7, 0, 1, slot(14), weights=wgt_first[:])
+        weave(woven1[0][:], pair(11, 14), 2)
+        gather(7, 1, 3, slot(9, 2))
+        weave(woven1[1][:], pair(12, 9), 2)
+        weave(woven1[2][:], pair(13, 10), 2)
+        early = quantise(woven0[:, 0 : 2 * W], "0", "wgt_first")
+        multiply(0, 0, early)
         multiply(1, 0, quantise(woven1[0][:], "10"))
-        multiply(0, 2, third)
         gelu(0)
-        gather(5, 3, 4, dst=last[:, 0, 1, :])
-        gather(6, 3, 4, dst=last[:, 1, 0, :])
-        gather(4, 3, 4, dst=last[:, 0, 0, :])
+        multiply(0, 1, early, NQ)
+        gather(6, 3, 4, slot(14))
+        multiply(0, 2, quantise(woven0[:, 2 * W : 3 * W], "02", "woven10"))
         multiply(1, 1, quantise(woven1[1][:], "11"))
+        gather(7, 3, 4, slot(9))
         multiply(1, 2, quantise(woven1[2][:], "12"))
         woven_last = tile("woven_last", [P, W], BF16, "codes_10")
+        last = slot(3, 12).rearrange("p (v w s) -> p v w s", v=2, s=NQ)[:, :, 5::-5, :]
         nc.scalar.copy(
             woven_last[:].rearrange("p (c i v u) -> p c v u i", i=4, v=2, u=2),
             last.rearrange("p v u (c i) -> p c v u i", i=4),
@@ -180,7 +178,7 @@ def tile_list_hboth_gelu_kernel(
         gelu(1)
         gelu(2)
         scatter(0, 1)
-        multiply(0, 3, quantise(woven0[:, 3 * W : 4 * W], "03", "flat1"))
+        multiply(0, 3, quantise(woven0[:, 3 * W : 4 * W], "03", "slots"))
         multiply(1, 3, quantise(woven_last[:], "13"))
         scatter(1, 3)
         gelu(3)

@@ -47,7 +47,7 @@ def tile_list_hboth_gelu_kernel(
         page = tile("page", [P, T], F32)
         planes = [tile("plane%d" % n, [P, T], F32) for n in range(PASSES * PACK)]
         picked0 = tile("picked0", [P, PACK, S], F32)
-        flat = tile("slots", [P, 17 * NQ], F32)
+        flat = tile("slots", [P, 16 * NQ], F32)
 
         def slot(s0, n=1):
             return flat[:, s0 * NQ : (s0 + n) * NQ]
@@ -148,34 +148,32 @@ def tile_list_hboth_gelu_kernel(
         for n in range(1, 4):
             gather(n, 0, 4, picked0[:, n, :])
         weave(woven0[:], picked0[:], 0)
-        gather(4, 0, 4, slot(5, 4))
-        gather(5, 0, 4, slot(0, 4))
+        gather(4, 0, 4, slot(6, 4))
+        gather(5, 0, 3, slot(10, 3))
         woven1 = [tile("woven1%d" % q, [P, W], BF16) for q in range(3)]
         for q in range(3):
-            weave(woven1[q][:], pair(q + 5, q), 0)
-        gather(6, 0, 3, slot(11, 3))
-        gather(7, 0, 1, slot(14), weights=wgt_first[:])
-        weave(woven1[0][:], pair(11, 14), 2)
-        gather(7, 1, 3, slot(9, 2))
-        weave(woven1[1][:], pair(12, 9), 2)
-        weave(woven1[2][:], pair(13, 10), 2)
-        early = quantise(woven0[:, 0 : 2 * W], "0", "wgt_first")
+            weave(woven1[q][:], pair(q + 6, q + 10), 0)
+        gather(6, 0, 3, slot(2, 3))
+        gather(7, 0, 1, slot(5), weights=wgt_first[:])
+        weave(woven1[0][:], pair(2, 5), 2)
+        gather(7, 1, 3, slot(0, 2))
+        weave(woven1[1][:], pair(3, 0), 2)
+        weave(woven1[2][:], pair(4, 1), 2)
+        early = quantise(woven0[:, 0 : 3 * W], "0", "wgt_first")
         multiply(0, 0, early)
         multiply(1, 0, quantise(woven1[0][:], "10"))
         gelu(0)
         multiply(0, 1, early, NQ)
-        gather(6, 3, 4, slot(14))
-        multiply(0, 2, quantise(woven0[:, 2 * W : 3 * W], "02", "woven10"))
-        multiply(1, 1, quantise(woven1[1][:], "11"))
-        gather(7, 3, 4, slot(9))
-        multiply(1, 2, quantise(woven1[2][:], "12"))
+        gather(5, 3, 4, slot(5))
         woven_last = tile("woven_last", [P, W], BF16, "codes_10")
-        last = slot(3, 12).rearrange("p (v w s) -> p v w s", v=2, s=NQ)[:, :, 5::-5, :]
-        nc.scalar.copy(
-            woven_last[:].rearrange("p (c i v u) -> p c v u i", i=4, v=2, u=2),
-            last.rearrange("p v u (c i) -> p c v u i", i=4),
-        )
+        weave(woven_last[:], pair(9, 5), 0)
+        multiply(1, 1, quantise(woven1[1][:], "11"))
+        multiply(0, 2, early, 2 * NQ)
         gelu(1)
+        gather(6, 3, 4, slot(0))
+        multiply(1, 2, quantise(woven1[2][:], "12"))
+        gather(7, 3, 4, slot(1))
+        weave(woven_last[:], pair(0, 1), 2)
         gelu(2)
         scatter(0, 1)
         multiply(0, 3, quantise(woven0[:, 3 * W : 4 * W], "03", "slots"))

@@ -159,7 +159,13 @@ def tile_list_hboth_gelu_kernel(
         gather(7, 1, 3, slot(0, 2))
         weave(woven1[1][:], pair(3, 0), 2)
         weave(woven1[2][:], pair(4, 1), 2)
-        early = quantise(woven0[:, 0 : 3 * W], "0", "wgt_first")
+        early = tile("codes_0", [P, 3 * NQ], U32, "wgt_first"), tile("scales_0", [P, 3 * NQ], U8)
+        for q0, q1 in ((0, 1), (1, 3)):
+            nc.vector.quantize_mx(
+                out=early[0][:, q0 * NQ : q1 * NQ].bitcast(E4M3),
+                scales=early[1][:, q0 * NQ : q1 * NQ],
+                in_=woven0[:, q0 * W : q1 * W],
+            )
         multiply(0, 0, early)
         multiply(1, 0, quantise(woven1[0][:], "10"))
         gelu(0)

@@ -20,10 +20,23 @@ GELU = mybir.ActivationFunctionType.Gelu_apprx_tanh
 P = 128
 T = 1024
 S = 512
-NQ = 128
+GROUP = 16
+QUARTERS = 4
+NQ = S // QUARTERS
 PASSES = 2
 PACK = 4
 W = NQ * PACK
+QUADRANT = 32
+SCALE_ROWS = 4
+RUN = 4
+PLANES_AHEAD = 3
+
+P7_Q1 = 0
+P6_Q0 = 2
+P7_Q0 = 5
+P4_Q0 = 6
+P5_Q0 = 10
+SLOTS = 16
 
 
 def tile_list_hboth_gelu_kernel(
@@ -37,36 +50,37 @@ def tile_list_hboth_gelu_kernel(
         def tile(name, shape, dtype, tag=None):
             return keep.tile(shape, dtype, name=name, tag=tag or name, align_bytes=64)
 
-        offs_t = keep.tile([P, S // 16], U16, name="offs_t")
-        offs2_t = keep.tile([P, S // 16], U16, name="offs2_t")
+        offs_t = keep.tile([P, S // GROUP], U16, name="offs_t")
+        offs2_t = keep.tile([P, S // GROUP], U16, name="offs2_t")
         b_t = keep.tile([P, 1], F32, name="b_t")
         wgt_t = tile("wgt_t", [P, S], F32)
         w4_t = tile("w4_t", [P, PASSES, 2 * P], U8)
         r8_t = tile("r8_t", [P, PASSES, P * PACK], U8)
-        sc_t = tile("sc_t", [P, 2 * PASSES, 4 * P], U8)
+        sc_t = tile("sc_t", [P, 2 * PASSES, SCALE_ROWS * P], U8)
         page = tile("page", [P, T], F32)
         planes = [tile("plane%d" % n, [P, T], F32) for n in range(PASSES * PACK)]
         picked0 = tile("picked0", [P, PACK, S], F32)
-        flat = tile("slots", [P, 16 * NQ], F32)
+        slots = tile("slots", [P, SLOTS * NQ], F32)
 
-        def slot(s0, n=1):
-            return flat[:, s0 * NQ : (s0 + n) * NQ]
+        def slot(first, count=1):
+            return slots[:, first * NQ : (first + count) * NQ]
 
-        def pair(s0, s1):
-            lo, step = min(s0, s1), abs(s1 - s0)
-            rows = slot(lo, 2 * step).rearrange("p (t s) -> p t s", t=2)[:, :, 0:NQ]
-            return rows if s0 < s1 else rows[:, ::-1, :]
+        def pair(upper, lower):
+            step = abs(lower - upper)
+            rows = slot(min(upper, lower), 2 * step).rearrange("p (t s) -> p t s", t=2)[:, :, 0:NQ]
+            return rows if upper < lower else rows[:, ::-1, :]
 
         wgt_first = tile("wgt_first", [P, NQ], F32)
         val = tile("val", [P, S], F32)
-        sums = [psum.tile([P, NQ], F32, name="sum%d" % q) for q in range(4)]
+        sums = [psum.tile([P, NQ], F32, name="sum%d" % q) for q in range(QUARTERS)]
 
         nc.vector.memset(sc_t[:, :, 0:P].bitcast(I32), 0)
         nc.vector.memset(page[:], 0.0)
-        warm = keep.tile([P, 1], F32, name="warm")
-        nc.scalar.activation(warm[:], page[:, 0:1], GELU)
+        warm = keep.tile([P, 2], F32, name="warm")
+        nc.gpsimd.memset(warm[:, 0:1], 0.0)
+        nc.scalar.activation(warm[:, 1:2], warm[:, 0:1], GELU)
 
-        x_view = xT.rearrange("(a p i) t -> a i p t", a=PASSES, p=P, i=PACK)
+        x_view = xT.rearrange("(a p t) c -> a t p c", a=PASSES, p=P, t=PACK)
 
         def load_plane(n):
             nc.sync.dma_start(out=planes[n][:], in_=x_view[n // PACK, n % PACK])
@@ -76,44 +90,44 @@ def tile_list_hboth_gelu_kernel(
         nc.scalar.copy(wgt_t[:, 0:NQ], wgt_first[:])
         nc.sync.dma_start(out=offs_t[:], in_=offs)
         nc.sync.dma_start(out=wgt_t[:, NQ:S], in_=wgt[:, NQ:S])
-        load_plane(1)
-        load_plane(2)
+        for n in range(1, PLANES_AHEAD):
+            load_plane(n)
         for which, scales in enumerate((w4_scales, r8_scales)):
             nc.sync.dma_start(
-                out=sc_t[0:P:32, which * PASSES : (which + 1) * PASSES, :].bitcast(I32),
-                in_=scales.rearrange("a (q r) n -> q a (r n)", r=4).bitcast(I32),
+                out=sc_t[0:P:QUADRANT, which * PASSES : (which + 1) * PASSES, :].bitcast(I32),
+                in_=scales.rearrange("a (u r) n -> u a (r n)", r=SCALE_ROWS).bitcast(I32),
             )
-        for n in range(3, 8):
+        for n in range(PLANES_AHEAD, PASSES * PACK):
             load_plane(n)
         nc.sync.dma_start(out=b_t[:], in_=b.rearrange("(p o) -> p o", o=1))
         nc.sync.dma_start(out=offs2_t[:], in_=offs2)
-        nc.sync.dma_start(out=r8_t[:].bitcast(I32), in_=r8_words.rearrange("a p n i -> p a (n i)").bitcast(I32))
+        nc.sync.dma_start(out=r8_t[:].bitcast(I32), in_=r8_words.rearrange("a p n t -> p a (n t)").bitcast(I32))
         nc.sync.dma_start(out=w4_t[:].bitcast(I32), in_=w4_words.rearrange("a p n -> p a n").bitcast(I32))
-        for r in range(1, 4):
+        for r in range(1, SCALE_ROWS):
             nc.sync.dma_start(
-                out=sc_t[r:P:32, :, 0:P].bitcast(I32), in_=sc_t[0:P:32, :, r * P : (r + 1) * P].bitcast(I32)
+                out=sc_t[r:P:QUADRANT, :, 0:P].bitcast(I32),
+                in_=sc_t[0:P:QUADRANT, :, r * P : (r + 1) * P].bitcast(I32),
             )
 
         def gather(n, q0, q1, dst, weights=None):
             j0, j1 = q0 * NQ, q1 * NQ
             nc.vector.tensor_tensor(
                 dst,
-                planes[n][:].indirect(offs_t[:, j0 // 16 : j1 // 16]),
+                planes[n][:].indirect(offs_t[:, j0 // GROUP : j1 // GROUP]),
                 wgt_t[:, j0:j1] if weights is None else weights,
                 MULT,
             )
 
         def weave(dst, src, t0):
             nc.scalar.activation(
-                dst.rearrange("p (c i t) -> p c t i", i=4, t=PACK)[:, :, t0 : t0 + src.shape[1], :],
-                src.rearrange("p t (c i) -> p c t i", i=4),
+                dst.rearrange("p (c i t) -> p c t i", i=RUN, t=PACK)[:, :, t0 : t0 + src.shape[1], :],
+                src.rearrange("p t (c i) -> p c t i", i=RUN),
                 COPY,
             )
 
         def quantise(src, name, tag=None):
-            n = src.shape[1] // PACK
-            codes = tile("codes_" + name, [P, n], U32, tag)
-            scales = tile("scales_" + name, [P, n], U8)
+            codes = tile("codes_" + name, [P, NQ], U32, tag)
+            scales = tile("scales_" + name, [P, NQ], U8)
             nc.vector.quantize_mx(out=codes[:].bitcast(E4M3), scales=scales[:], in_=src)
             return codes, scales
 
@@ -137,30 +151,33 @@ def tile_list_hboth_gelu_kernel(
         def scatter(q0, q1):
             j0, j1 = q0 * NQ, q1 * NQ
             nc.vector.tensor_tensor(
-                page[:].indirect(offs2_t[:, j0 // 16 : j1 // 16]), val[:, j0:j1], wgo_t[:, j0:j1], MULT
+                page[:].indirect(offs2_t[:, j0 // GROUP : j1 // GROUP]), val[:, j0:j1], wgo_t[:, j0:j1], MULT
             )
 
         gather(0, 0, 1, picked0[:, 0, 0:NQ], weights=wgt_first[:])
-        gather(0, 1, 4, picked0[:, 0, NQ:S])
+        gather(0, 1, QUARTERS, picked0[:, 0, NQ:S])
         wgo_t = tile("wgo_t", [P, S], F32, "plane0")
         nc.sync.dma_start(out=wgo_t[:], in_=wgo)
-        woven0 = tile("woven0", [P, 4 * W], BF16)
-        for n in range(1, 4):
-            gather(n, 0, 4, picked0[:, n, :])
+        woven0 = tile("woven0", [P, QUARTERS * W], BF16)
+        for n in range(1, PACK):
+            gather(n, 0, QUARTERS, picked0[:, n, :])
         weave(woven0[:], picked0[:], 0)
-        gather(4, 0, 4, slot(6, 4))
-        gather(5, 0, 3, slot(10, 3))
-        woven1 = [tile("woven1%d" % q, [P, W], BF16) for q in range(3)]
-        for q in range(3):
-            weave(woven1[q][:], pair(q + 6, q + 10), 0)
-        gather(6, 0, 3, slot(2, 3))
-        gather(7, 0, 1, slot(5), weights=wgt_first[:])
-        weave(woven1[0][:], pair(2, 5), 2)
-        gather(7, 1, 3, slot(0, 2))
-        weave(woven1[1][:], pair(3, 0), 2)
-        weave(woven1[2][:], pair(4, 1), 2)
-        early = tile("codes_0", [P, 3 * NQ], U32, "wgt_first"), tile("scales_0", [P, 3 * NQ], U8)
-        for q0, q1 in ((0, 1), (1, 3)):
+
+        last = QUARTERS - 1
+        gather(4, 0, QUARTERS, slot(P4_Q0, QUARTERS))
+        gather(5, 0, last, slot(P5_Q0, last))
+        woven1 = [tile("woven1%d" % q, [P, W], BF16) for q in range(last)]
+        for q in range(last):
+            weave(woven1[q][:], pair(P4_Q0 + q, P5_Q0 + q), 0)
+        gather(6, 0, last, slot(P6_Q0, last))
+        gather(7, 0, 1, slot(P7_Q0), weights=wgt_first[:])
+        weave(woven1[0][:], pair(P6_Q0, P7_Q0), 2)
+        gather(7, 1, last, slot(P7_Q1, last - 1))
+        for q in range(1, last):
+            weave(woven1[q][:], pair(P6_Q0 + q, P7_Q1 + q - 1), 2)
+
+        early = tile("codes_0", [P, last * NQ], U32, "wgt_first"), tile("scales_0", [P, last * NQ], U8)
+        for q0, q1 in ((0, 1), (1, last)):
             nc.vector.quantize_mx(
                 out=early[0][:, q0 * NQ : q1 * NQ].bitcast(E4M3),
                 scales=early[1][:, q0 * NQ : q1 * NQ],
@@ -170,21 +187,23 @@ def tile_list_hboth_gelu_kernel(
         multiply(1, 0, quantise(woven1[0][:], "10"))
         gelu(0)
         multiply(0, 1, early, NQ)
-        gather(5, 3, 4, slot(5))
+
+        gather(5, last, QUARTERS, slot(P7_Q0))
         woven_last = tile("woven_last", [P, W], BF16, "codes_10")
-        weave(woven_last[:], pair(9, 5), 0)
+        weave(woven_last[:], pair(P4_Q0 + last, P7_Q0), 0)
         multiply(1, 1, quantise(woven1[1][:], "11"))
         multiply(0, 2, early, 2 * NQ)
         gelu(1)
-        gather(6, 3, 4, slot(0))
+        gather(6, last, QUARTERS, slot(P7_Q1))
         multiply(1, 2, quantise(woven1[2][:], "12"))
-        gather(7, 3, 4, slot(1))
-        weave(woven_last[:], pair(0, 1), 2)
+        gather(7, last, QUARTERS, slot(P7_Q1 + 1))
+        weave(woven_last[:], pair(P7_Q1, P7_Q1 + 1), 2)
         gelu(2)
+
         scatter(0, 1)
-        multiply(0, 3, quantise(woven0[:, 3 * W : 4 * W], "03", "slots"))
-        multiply(1, 3, quantise(woven_last[:], "13"))
-        scatter(1, 3)
-        gelu(3)
-        scatter(3, 4)
+        multiply(0, last, quantise(woven0[:, last * W : QUARTERS * W], "03", "slots"))
+        multiply(1, last, quantise(woven_last[:], "13"))
+        scatter(1, last)
+        gelu(last)
+        scatter(last, QUARTERS)
         nc.sync.dma_start(out=out, in_=page[:])

@@ -14,7 +14,6 @@ E4M3 = mybir.dt.float8_e4m3fn_x4
 E2M1 = mybir.dt.float4_e2m1fn_x4
 
 MULT = mybir.AluOpType.mult
-COPY = mybir.ActivationFunctionType.Copy
 GELU = mybir.ActivationFunctionType.Gelu_apprx_tanh
 
 P = 128
@@ -34,9 +33,7 @@ PLANES_AHEAD = 3
 P7_Q1 = 0
 P6_Q0 = 2
 P7_Q0 = 5
-P4_Q0 = 6
-P5_Q0 = 10
-SLOTS = 16
+SLOTS = 10
 
 
 def tile_list_hboth_gelu_kernel(
@@ -60,6 +57,7 @@ def tile_list_hboth_gelu_kernel(
         page = tile("page", [P, T], F32)
         planes = [tile("plane%d" % n, [P, T], F32) for n in range(PASSES * PACK)]
         picked0 = tile("picked0", [P, PACK, S], F32)
+        picked45 = tile("picked45", [P, 2, S], F32)
         slots = tile("slots", [P, SLOTS * NQ], F32)
 
         def slot(first, count=1):
@@ -118,12 +116,14 @@ def tile_list_hboth_gelu_kernel(
                 MULT,
             )
 
-        def weave(dst, src, t0):
-            nc.scalar.activation(
+        def woven_views(dst, src, t0):
+            return (
                 dst.rearrange("p (c i t) -> p c t i", i=RUN, t=PACK)[:, :, t0 : t0 + src.shape[1], :],
                 src.rearrange("p t (c i) -> p c t i", i=RUN),
-                COPY,
             )
+
+        def weave(dst, src, t0):
+            nc.scalar.copy(*woven_views(dst, src, t0))
 
         def quantise(src, name, tag=None):
             codes = tile("codes_" + name, [P, NQ], U32, tag)
@@ -164,11 +164,11 @@ def tile_list_hboth_gelu_kernel(
         weave(woven0[:], picked0[:], 0)
 
         last = QUARTERS - 1
-        gather(4, 0, QUARTERS, slot(P4_Q0, QUARTERS))
-        gather(5, 0, last, slot(P5_Q0, last))
+        for t in range(2):
+            gather(PACK + t, 0, QUARTERS, picked45[:, t, :])
         woven1 = [tile("woven1%d" % q, [P, W], BF16) for q in range(last)]
         for q in range(last):
-            weave(woven1[q][:], pair(P4_Q0 + q, P5_Q0 + q), 0)
+            weave(woven1[q][:], picked45[:, :, q * NQ : (q + 1) * NQ], 0)
         gather(6, 0, last, slot(P6_Q0, last))
         gather(7, 0, 1, slot(P7_Q0), weights=wgt_first[:])
         weave(woven1[0][:], pair(P6_Q0, P7_Q0), 2)
@@ -188,20 +188,19 @@ def tile_list_hboth_gelu_kernel(
         gelu(0)
         multiply(0, 1, early, NQ)
 
-        gather(5, last, QUARTERS, slot(P7_Q0))
+        gather(6, last, QUARTERS, slot(P7_Q0))
         woven_last = tile("woven_last", [P, W], BF16, "codes_10")
-        weave(woven_last[:], pair(P4_Q0 + last, P7_Q0), 0)
+        weave(woven_last[:], picked45[:, :, last * NQ : S], 0)
         multiply(1, 1, quantise(woven1[1][:], "11"))
         multiply(0, 2, early, 2 * NQ)
         gelu(1)
-        gather(6, last, QUARTERS, slot(P7_Q1))
+        gather(7, last, QUARTERS, slot(P7_Q1))
         multiply(1, 2, quantise(woven1[2][:], "12"))
-        gather(7, last, QUARTERS, slot(P7_Q1 + 1))
-        weave(woven_last[:], pair(P7_Q1, P7_Q1 + 1), 2)
+        weave(woven_last[:], pair(P7_Q0, P7_Q1), 2)
         gelu(2)
+        multiply(0, last, quantise(woven0[:, last * W : QUARTERS * W], "03", "woven11"))
 
         scatter(0, 1)
-        multiply(0, last, quantise(woven0[:, last * W : QUARTERS * W], "03", "slots"))
         multiply(1, last, quantise(woven_last[:], "13"))
         scatter(1, last)
         gelu(last)

from contextlib import ExitStack

import concourse.mybir as mybir

FLOPS = 268435456

F32 = mybir.dt.float32
BF16 = mybir.dt.bfloat16
U8 = mybir.dt.uint8
U16 = mybir.dt.uint16
U32 = mybir.dt.uint32
I32 = mybir.dt.int32
E4M3 = mybir.dt.float8_e4m3fn_x4
E2M1 = mybir.dt.float4_e2m1fn_x4

MULT = mybir.AluOpType.mult
GELU = mybir.ActivationFunctionType.Gelu_apprx_tanh

P = 128
T = 1024
S = 512
GROUP = 16
QUARTERS = 4
NQ = S // QUARTERS
PASSES = 2
PACK = 4
W = NQ * PACK
QUADRANT = 32
SCALE_ROWS = 4
RUN = 4
PLANES_AHEAD = 3

P7_Q1 = 0
P6_Q0 = 2
P7_Q0 = 5
SLOTS = 10


def tile_list_hboth_gelu_kernel(
    tc, xT, w4_words, w4_scales, r8_words, r8_scales, wgt, b, wgo, offs, offs2, out
):
    nc = tc.nc
    with ExitStack() as ctx:
        keep = ctx.enter_context(tc.tile_pool(name="keep", bufs=1))
        psum = ctx.enter_context(tc.psum_pool(name="psum", bufs=1))

        def tile(name, shape, dtype, tag=None):
            return keep.tile(shape, dtype, name=name, tag=tag or name, align_bytes=64)

        offs_t = keep.tile([P, S // GROUP], U16, name="offs_t")
        offs2_t = keep.tile([P, S // GROUP], U16, name="offs2_t")
        b_t = keep.tile([P, 1], F32, name="b_t")
        wgt_t = tile("wgt_t", [P, S], F32)
        w4_t = tile("w4_t", [P, PASSES, 2 * P], U8)
        r8_t = tile("r8_t", [P, PASSES, P * PACK], U8)
        sc_t = tile("sc_t", [P, 2 * PASSES, SCALE_ROWS * P], U8)
        page = tile("page", [P, T], F32)
        planes = [tile("plane%d" % n, [P, T], F32) for n in range(PASSES * PACK)]
        picked0 = tile("picked0", [P, PACK, S], F32)
        picked45 = tile("picked45", [P, 2, S], F32)
        slots = tile("slots", [P, SLOTS * NQ], F32)

        def slot(first, count=1):
            return slots[:, first * NQ : (first + count) * NQ]

        def pair(upper, lower):
            step = abs(lower - upper)
            rows = slot(min(upper, lower), 2 * step).rearrange("p (t s) -> p t s", t=2)[:, :, 0:NQ]
            return rows if upper < lower else rows[:, ::-1, :]

        wgt_first = tile("wgt_first", [P, NQ], F32)
        val = tile("val", [P, S], F32)
        sums = [psum.tile([P, NQ], F32, name="sum%d" % q) for q in range(QUARTERS)]

        nc.vector.memset(sc_t[:, :, 0:P].bitcast(I32), 0)
        nc.vector.memset(page[:], 0.0)
        warm = keep.tile([P, 2], F32, name="warm")
        nc.gpsimd.memset(warm[:, 0:1], 0.0)
        nc.scalar.activation(warm[:, 1:2], warm[:, 0:1], GELU)

        x_view = xT.rearrange("(a p t) c -> a t p c", a=PASSES, p=P, t=PACK)

        def load_plane(n):
            nc.sync.dma_start(out=planes[n][:], in_=x_view[n // PACK, n % PACK])

        load_plane(0)
        nc.scalar.dma_start(out=wgt_first[:], in_=wgt[:, 0:NQ])
        nc.scalar.copy(wgt_t[:, 0:NQ], wgt_first[:])
        nc.sync.dma_start(out=offs_t[:], in_=offs)
        nc.sync.dma_start(out=wgt_t[:, NQ:S], in_=wgt[:, NQ:S])
        for n in range(1, PLANES_AHEAD):
            load_plane(n)
        for which, scales in enumerate((w4_scales, r8_scales)):
            nc.sync.dma_start(
                out=sc_t[0:P:QUADRANT, which * PASSES : (which + 1) * PASSES, :].bitcast(I32),
                in_=scales.rearrange("a (u r) n -> u a (r n)", r=SCALE_ROWS).bitcast(I32),
            )
        for n in range(PLANES_AHEAD, PASSES * PACK):
            load_plane(n)
        nc.sync.dma_start(out=b_t[:], in_=b.rearrange("(p o) -> p o", o=1))
        nc.sync.dma_start(out=offs2_t[:], in_=offs2)
        nc.sync.dma_start(out=r8_t[:].bitcast(I32), in_=r8_words.rearrange("a p n t -> p a (n t)").bitcast(I32))
        nc.sync.dma_start(out=w4_t[:].bitcast(I32), in_=w4_words.rearrange("a p n -> p a n").bitcast(I32))
        for r in range(1, SCALE_ROWS):
            nc.sync.dma_start(
                out=sc_t[r:P:QUADRANT, :, 0:P].bitcast(I32),
                in_=sc_t[0:P:QUADRANT, :, r * P : (r + 1) * P].bitcast(I32),
            )

        def gather(n, q0, q1, dst, weights=None):
            j0, j1 = q0 * NQ, q1 * NQ
            nc.vector.tensor_tensor(
                dst,
                planes[n][:].indirect(offs_t[:, j0 // GROUP : j1 // GROUP]),
                wgt_t[:, j0:j1] if weights is None else weights,
                MULT,
            )

        def woven_views(dst, src, t0):
            return (
                dst.rearrange("p (c i t) -> p c t i", i=RUN, t=PACK)[:, :, t0 : t0 + src.shape[1], :],
                src.rearrange("p t (c i) -> p c t i", i=RUN),
            )

        def weave(dst, src, t0):
            nc.scalar.copy(*woven_views(dst, src, t0))

        def quantise(src, name, tag=None):
            codes = tile("codes_" + name, [P, NQ], U32, tag)
            scales = tile("scales_" + name, [P, NQ], U8)
            nc.vector.quantize_mx(out=codes[:].bitcast(E4M3), scales=scales[:], in_=src)
            return codes, scales

        def multiply(a, q, operand, c0=0):
            codes, scales = operand
            cols = slice(c0, c0 + NQ)
            for which, words in enumerate((w4_t[:, a, :].bitcast(E2M1), r8_t[:, a, :].bitcast(E4M3))):
                nc.tensor.matmul_mx(
                    out=sums[q][:],
                    lhsT=words,
                    lhsT_scale=sc_t[:, which * PASSES + a, 0:P],
                    rhs=codes[:, cols].bitcast(E4M3),
                    rhs_scale=scales[:, cols],
                    start=a == 0 and which == 0,
                    stop=a == 1 and which == 1,
                )

        def gelu(q):
            nc.scalar.activation(val[:, q * NQ : (q + 1) * NQ], sums[q][:], GELU, bias=b_t[:, 0:1])

        def scatter(q0, q1):
            j0, j1 = q0 * NQ, q1 * NQ
            nc.vector.tensor_tensor(
                page[:].indirect(offs2_t[:, j0 // GROUP : j1 // GROUP]), val[:, j0:j1], wgo_t[:, j0:j1], MULT
            )

        gather(0, 0, 1, picked0[:, 0, 0:NQ], weights=wgt_first[:])
        gather(0, 1, QUARTERS, picked0[:, 0, NQ:S])
        wgo_t = tile("wgo_t", [P, S], F32, "plane0")
        nc.sync.dma_start(out=wgo_t[:], in_=wgo)
        woven0 = tile("woven0", [P, QUARTERS * W], BF16)
        for n in range(1, PACK):
            gather(n, 0, QUARTERS, picked0[:, n, :])
        weave(woven0[:], picked0[:], 0)

        last = QUARTERS - 1
        for t in range(2):
            gather(PACK + t, 0, QUARTERS, picked45[:, t, :])
        woven1 = [tile("woven1%d" % q, [P, W], BF16) for q in range(last)]
        for q in range(last):
            weave(woven1[q][:], picked45[:, :, q * NQ : (q + 1) * NQ], 0)
        gather(6, 0, last, slot(P6_Q0, last))
        gather(7, 0, 1, slot(P7_Q0), weights=wgt_first[:])
        weave(woven1[0][:], pair(P6_Q0, P7_Q0), 2)
        gather(7, 1, last, slot(P7_Q1, last - 1))
        for q in range(1, last):
            weave(woven1[q][:], pair(P6_Q0 + q, P7_Q1 + q - 1), 2)

        early = tile("codes_0", [P, last * NQ], U32, "wgt_first"), tile("scales_0", [P, last * NQ], U8)
        for q0, q1 in ((0, 1), (1, last)):
            nc.vector.quantize_mx(
                out=early[0][:, q0 * NQ : q1 * NQ].bitcast(E4M3),
                scales=early[1][:, q0 * NQ : q1 * NQ],
                in_=woven0[:, q0 * W : q1 * W],
            )
        multiply(0, 0, early)
        multiply(1, 0, quantise(woven1[0][:], "10"))
        gelu(0)
        multiply(0, 1, early, NQ)

        gather(6, last, QUARTERS, slot(P7_Q0))
        woven_last = tile("woven_last", [P, W], BF16, "codes_10")
        weave(woven_last[:], picked45[:, :, last * NQ : S], 0)
        multiply(1, 1, quantise(woven1[1][:], "11"))
        multiply(0, 2, early, 2 * NQ)
        gelu(1)
        gather(7, last, QUARTERS, slot(P7_Q1))
        multiply(1, 2, quantise(woven1[2][:], "12"))
        weave(woven_last[:], pair(P7_Q0, P7_Q1), 2)
        gelu(2)
        multiply(0, last, quantise(woven0[:, last * W : QUARTERS * W], "03", "woven11"))

        scatter(0, 1)
        multiply(1, last, quantise(woven_last[:], "13"))
        scatter(1, last)
        gelu(last)
        scatter(last, QUARTERS)
        nc.sync.dma_start(out=out, in_=page[:])
